import numpy as np
import ml_dtypes


def mxq(x, axis, fmt="e4m3"):
    dtype, down = {"e4m3": (ml_dtypes.float8_e4m3fn, 7), "e5m2": (ml_dtypes.float8_e5m2, 14)}[fmt]
    v = np.moveaxis(np.asarray(x, np.float32).astype(ml_dtypes.bfloat16).astype(np.float64), axis, -1)
    blocks = v.reshape(v.shape[:-1] + (-1, 32))
    amax = np.abs(blocks).max(-1, keepdims=True)
    byte = np.maximum(np.where(amax > 0, np.frexp(amax)[1] - 1 + 127, 0) - down, 1)
    scale = np.exp2(byte - 127.0)
    codes = (blocks / scale).astype(np.float32).astype(dtype).astype(np.float64)
    return np.moveaxis((codes * scale).reshape(v.shape), -1, axis)


WIDE = False


def mx_kscale(k):
    if not WIDE:
        return np.ones(k)
    levels = np.array([10, -10, 5, -5, 0])
    if k % 512:
        return np.exp2(np.random.permutation(np.resize(levels, k // 32))).repeat(32)
    a = np.empty((k // 512, 16))
    for p in range(k // 512):
        a[p, :8] = np.random.permutation(np.resize(levels, 8))
        for g in range(8):
            far = levels[np.abs(levels - a[p, g]) >= 10]
            a[p, g + 8] = far[np.random.randint(len(far))]
    return np.exp2(a.ravel()).repeat(32)


def f64(x):
    return np.asarray(x).astype(np.float64)


def striped(idx):
    return np.tile(idx.reshape(-1, 16).T, (8, 1)).astype(np.uint16)


def unstriped(offs):
    return offs[:16].T.reshape(-1).astype(np.int64)


def pack_weight(w):
    k, n = w.shape
    w = f64(np.asarray(w, np.float32).astype(ml_dtypes.bfloat16)).reshape(k // 32, 32, n)
    amax = np.abs(w).max(1)
    byte = np.clip(np.where(amax > 0, np.frexp(amax)[1] - 1 + 127 - 7, 1), 1, 254)
    scaled = (w * np.exp2(127.0 - byte)[:, None, :]).reshape(k, n).astype(np.float32)
    words = np.ascontiguousarray(scaled.reshape(k // 512, 128, 4, n).transpose(0, 1, 3, 2)).astype(ml_dtypes.float8_e4m3fn).view(np.uint8)
    return words, np.ascontiguousarray(byte.astype(np.uint8).reshape(k // 512, 16, n))


def unpack_weight(words, scales):
    g, p, n, _ = words.shape
    vals = np.ascontiguousarray(words).view(ml_dtypes.float8_e4m3fn).astype(np.float64) * np.repeat(np.exp2(scales.astype(np.float64) - 127.0), 8, axis=1)[..., None]
    return vals.transpose(0, 1, 3, 2).reshape(g * 512, n)


E2M1 = np.array([0.0, 0.5, 1.0, 1.5, 2.0, 3.0, 4.0, 6.0, -0.0, -0.5, -1.0, -1.5, -2.0, -3.0, -4.0, -6.0])


def pack_fp4(w):
    k, n = w.shape
    w = f64(np.asarray(w, np.float32).astype(ml_dtypes.bfloat16)).reshape(k // 32, 32, n)
    amax = np.abs(w).max(1)
    mant, ex = np.frexp(amax / 6.0)
    byte = np.clip(np.where(amax > 0, np.where(mant > 0.5, ex, ex - 1) + 127, 1), 1, 254)
    scaled = (w * np.exp2(127.0 - byte)[:, None, :]).reshape(k, n).astype(np.float32)
    c = np.ascontiguousarray(scaled.reshape(k // 512, 128, 4, n).transpose(0, 1, 3, 2)).astype(ml_dtypes.float4_e2m1fn).view(np.uint8) & 0xF
    words = (c[..., 0::2] | (c[..., 1::2] << 4)).reshape(k // 512, 128, 2 * n)
    return np.ascontiguousarray(words), np.ascontiguousarray(byte.astype(np.uint8).reshape(k // 512, 16, n))


def unpack_fp4(words, scales):
    g, _, n = scales.shape
    words = np.ascontiguousarray(words).reshape(g, 128, n, 2)
    nib = np.empty((g, 128, n, 4), np.uint8)
    nib[..., 0::2] = words & 0xF
    nib[..., 1::2] = words >> 4
    vals = E2M1[nib] * np.repeat(np.exp2(scales.astype(np.float64) - 127.0), 8, axis=1)[..., None]
    return vals.transpose(0, 1, 3, 2).reshape(g * 512, n)


def gelu(v):
    return 0.5 * v * (1.0 + np.tanh(np.sqrt(2.0 / np.pi) * (v + 0.044715 * v**3)))

def planes(y):
    n, m = y.shape
    v = y.astype(np.float32).astype(ml_dtypes.bfloat16).astype(np.float64).reshape(n // 32, 32, m)
    top = np.abs(v).max(1)
    byte = np.clip(np.where(top > 0, np.frexp(top)[1] - 1 + 127 - 7, 1), 1, 254)
    codes = (v * np.exp2(127.0 - byte)[:, None, :]).reshape(n, m).astype(np.float32).astype(ml_dtypes.float8_e4m3fn).view(np.uint8)
    words = codes.reshape(n // 512, 128, 4, m).transpose(0, 1, 3, 2)
    return np.ascontiguousarray(words), np.ascontiguousarray(byte.astype(np.uint8).reshape(n // 512, 16, m))


K, T, S, H = 512, 1024, 512, 512


def setup_inputs():
    n = np.random.standard_normal
    s = mx_kscale(K)[:, None]
    u = mx_kscale(H)
    packed_xT = pack_weight(n((K, T)) * s)
    packed_w1 = pack_fp4(n((K, H)) / np.sqrt(2 * K) / s)
    packed_w3 = pack_fp4(n((H, H)) / np.sqrt(2 * H) / u[:, None])
    return {
        "x_words": packed_xT[0],
        "x_scales": packed_xT[1],
        "w1_words": packed_w1[0],
        "w1_scales": packed_w1[1],
        "w2": (n((K, H)) / np.sqrt(K) / s * u).astype(np.float32),
        "w3_words": packed_w3[0],
        "w3_scales": packed_w3[1],
        "offs": striped(np.random.permutation(T)[:S]),
    }


def reference(x_words, x_scales, w1_words, w1_scales, w2, w3_words, w3_scales, offs):
    xq = unpack_weight(x_words, x_scales)[:, unstriped(offs)]
    h = gelu(mxq(f64(w2), 0, "e4m3").T @ xq)
    out_0 = unpack_fp4(w1_words, w1_scales).T @ xq + unpack_fp4(w3_words, w3_scales).T @ mxq(h, 0, "e4m3")
    return (out_0,) + planes(out_0)

@@ -1,0 +1,179 @@
+from contextlib import ExitStack
+
+import concourse.mybir as mybir
+
+K, T, S, H = 512, 1024, 512, 512
+FLOPS = 3 * 2 * K * H * S
+
+F32 = mybir.dt.float32
+BF16 = mybir.dt.bfloat16
+I32 = mybir.dt.int32
+U32 = mybir.dt.uint32
+U16 = mybir.dt.uint16
+U8 = mybir.dt.uint8
+FP8X4 = mybir.dt.float8_e4m3fn_x4
+FP4X4 = mybir.dt.float4_e2m1fn_x4
+GELU = mybir.ActivationFunctionType.Gelu_apprx_tanh
+
+P = 128
+PACK = 4
+CHUNK = 128
+CHUNKS = S // CHUNK
+SCALAR_M = 24
+
+
+def tile_picked_lora_gelu_po_kernel(
+    tc, x_words, x_scales, w1_words, w1_scales, w2, w3_words, w3_scales, offs, out_0, out_1, out_2
+):
+    nc = tc.nc
+    with ExitStack() as ctx:
+        keep = ctx.enter_context(tc.tile_pool(name="keep", bufs=1))
+        psum = ctx.enter_context(tc.psum_pool(name="psum", bufs=1))
+
+        offsets = keep.tile([P, S // 16], U16, name="offsets")
+        x_table = keep.tile([P, T], I32, name="x_table", align_bytes=64)
+        x_scale_table = keep.tile([P, T], U8, name="x_scale_table", align_bytes=64)
+        w2_rows = [keep.tile([P, 2, H], F32, name="w2_rows%d" % u, align_bytes=64) for u in range(2)]
+        w_words = keep.tile([P, 2, 2 * H], U8, name="w_words", align_bytes=64)
+        w_scales = keep.tile([P, 2, H], U8, name="w_scales", tag="w_scales", align_bytes=64)
+        warm = keep.tile([P, 2], F32, name="warm")
+
+        nc.vector.memset(x_scale_table[:].bitcast(I32), 0)
+        nc.vector.memset(warm[:, 0:1], 0.0)
+        nc.vector.memset(w_scales[:].rearrange("p w c -> p (w c)").bitcast(I32), 0)
+
+        def load_scales(queue, tile, scales, quadrants):
+            for q in quadrants:
+                queue.dma_start(tile[32 * q : 32 * q + 4, :].bitcast(I32), scales[0, 4 * q : 4 * q + 4, :].bitcast(I32))
+
+        w2_view = w2.rearrange("(p j) c -> p j c", j=PACK)
+        nc.sync.dma_start(offsets[:], offs)
+        load_scales(nc.scalar, x_scale_table, x_scales, range(4))
+        nc.scalar.activation(warm[:, 1:2], warm[:, 0:1], GELU)
+        nc.sync.dma_start(w_words[:, 0, :].bitcast(I32), w1_words[0].bitcast(I32))
+        nc.sync.dma_start(w_words[:, 1, :].bitcast(I32), w3_words[0].bitcast(I32))
+        for u in range(2):
+            nc.sync.dma_start(w2_rows[u][:], w2_view[:, 2 * u : 2 * u + 2, :])
+        nc.sync.dma_start(x_table[:], x_words[0].rearrange("p n r -> p (n r)").bitcast(I32))
+        load_scales(nc.gpsimd, w_scales[:, 0, :], w1_scales, range(2))
+        load_scales(nc.sync, w_scales[:, 0, :], w1_scales, range(2, 4))
+        load_scales(nc.sync, w_scales[:, 1, :], w3_scales, range(4))
+
+        dealt_words = keep.tile([P, PACK, 2, 2 * P], U8, name="dealt_words", align_bytes=64)
+        nc.vector.tensor_copy(
+            dealt_words[:].rearrange("p t w (g m b) -> p (w g) t m b", m=8, b=2),
+            w_words[:].rearrange("p w (g m t b) -> p (w g) t m b", m=8, t=PACK, b=2),
+        )
+
+        x_codes = keep.tile([P, S], U32, name="x_codes", align_bytes=64)
+        x_plane = keep.tile([P, S], U8, name="x_plane", align_bytes=64)
+        nc.vector.tensor_copy(x_plane[:], x_scale_table[:].indirect(offsets[:]))
+
+        w2_bf = keep.tile([P, PACK * H], BF16, name="w2_bf", align_bytes=64)
+        w2_dst = w2_bf[:].rearrange("p (t g m j) -> p g t m j", t=PACK, m=2, j=PACK)
+        srcs = [w2_rows[u][:].rearrange("p j (g m t) -> p g t m j", m=2, t=PACK) for u in range(2)]
+        nc.scalar.copy(w2_dst[:, :, :, :, 0:2], srcs[0])
+        cut = SCALAR_M // 2
+        nc.scalar.copy(w2_dst[:, :cut, :, :, 2:4], srcs[1][:, :cut])
+        nc.vector.tensor_copy(w2_dst[:, cut:, :, :, 2:4], srcs[1][:, cut:])
+        w2_codes = keep.tile([P, H], U32, name="w2_codes", align_bytes=64)
+        w2_plane = keep.tile([P, H], U8, name="w2_plane", align_bytes=64)
+        for t in range(PACK):
+            cols = slice(t * P, (t + 1) * P)
+            nc.vector.quantize_mx(
+                out=w2_codes[:, cols].bitcast(FP8X4),
+                scales=w2_plane[:, cols],
+                in_=w2_bf[:, t * PACK * P : (t + 1) * PACK * P],
+            )
+
+        for c in range(CHUNKS):
+            nc.vector.tensor_copy(
+                x_codes[:, c * CHUNK : (c + 1) * CHUNK],
+                x_table[:].bitcast(U32).indirect(offsets[:, c * CHUNK // 16 : (c + 1) * CHUNK // 16]),
+            )
+
+        h_bf = []
+        for c in range(CHUNKS):
+            tokens = slice(c * CHUNK, (c + 1) * CHUNK)
+            pre = psum.tile([P, PACK, CHUNK], F32, name="pre%d" % c, tag="pre%d" % c)
+            for t in range(PACK):
+                cols = slice(t * P, (t + 1) * P)
+                nc.tensor.matmul_mx(
+                    out=pre[:, t, :],
+                    lhsT=w2_codes[:, cols].bitcast(FP8X4),
+                    lhsT_scale=w2_plane[:, cols],
+                    rhs=x_codes[:, tokens].bitcast(FP8X4),
+                    rhs_scale=x_plane[:, tokens],
+                    start=True,
+                    stop=True,
+                )
+            hb = keep.tile([P, CHUNK * PACK], BF16, name="h_bf%d" % c, align_bytes=64)
+            nc.scalar.activation(hb[:].rearrange("p (n t) -> p n t", t=PACK), pre[:].rearrange("p t n -> p n t"), GELU)
+            h_bf.append(hb)
+
+        dealt_scales = keep.tile([P, PACK, 2, P], U8, name="dealt_scales", align_bytes=64)
+        nc.vector.tensor_copy(
+            dealt_scales[:].rearrange("p t w (g m) -> p (w g) t m", m=16),
+            w_scales[:].rearrange("p w (g m t) -> p (w g) t m", m=16, t=PACK),
+        )
+
+        y_codes = keep.tile([P, S], I32, name="y_codes", align_bytes=64)
+        y_plane = keep.tile([P, S], U8, name="y_plane", align_bytes=64)
+        out_view = out_0.rearrange("(p t) j -> p t j", t=PACK)
+        codes_view = out_1[0].rearrange("p n r -> p (n r)").bitcast(I32)
+
+        h_codes = keep.tile([P, S], U32, name="h_codes", align_bytes=64)
+        h_plane = keep.tile([P, S], U8, name="h_plane", tag="w_scales", align_bytes=64)
+        for c in range(CHUNKS):
+            tokens = slice(c * CHUNK, (c + 1) * CHUNK)
+            nc.vector.quantize_mx(out=h_codes[:, tokens].bitcast(FP8X4), scales=h_plane[:, tokens], in_=h_bf[c][:])
+
+        for c in range(CHUNKS):
+            tokens = slice(c * CHUNK, (c + 1) * CHUNK)
+            last = c == CHUNKS - 1
+            if last:
+                low = psum.tile([P, 2, CHUNK], F32, name="low", tag="pre0")
+                high = psum.tile([P, 2, CHUNK], F32, name="high")
+                slots = [low[:, 0, :], low[:, 1, :], high[:, 0, :], high[:, 1, :]]
+            else:
+                acc = psum.tile([P, PACK, CHUNK], F32, name="acc%d" % c)
+                slots = [acc[:, t, :] for t in range(PACK)]
+            for t in range(PACK):
+                nc.tensor.matmul_mx(
+                    out=slots[t],
+                    lhsT=dealt_words[:, t, 0, :].bitcast(FP4X4),
+                    lhsT_scale=dealt_scales[:, t, 0, :],
+                    rhs=x_codes[:, tokens].bitcast(FP8X4),
+                    rhs_scale=x_plane[:, tokens],
+                    start=True,
+                    stop=False,
+                )
+                nc.tensor.matmul_mx(
+                    out=slots[t],
+                    lhsT=dealt_words[:, t, 1, :].bitcast(FP4X4),
+                    lhsT_scale=dealt_scales[:, t, 1, :],
+                    rhs=h_codes[:, tokens].bitcast(FP8X4),
+                    rhs_scale=h_plane[:, tokens],
+                    start=False,
+                    stop=True,
+                )
+            y = keep.tile([P, PACK, CHUNK], F32, name="y%d" % c, align_bytes=64)
+            if last:
+                nc.scalar.copy(y[:, 0:2, :], low[:])
+                nc.vector.tensor_copy(y[:, 2:4, :], high[:])
+            else:
+                nc.scalar.copy(y[:], acc[:])
+            nc.sync.dma_start(out_view[:, :, tokens], y[:])
+            y_bf = keep.tile([P, CHUNK * PACK], BF16, name="y_bf%d" % c, align_bytes=64)
+            nc.vector.tensor_copy(
+                y_bf[:].rearrange("p (g i t) -> p g t i", i=4, t=PACK),
+                y[:].rearrange("p t (g i) -> p g t i", i=4),
+            )
+            nc.vector.quantize_mx(out=y_codes[:, tokens].bitcast(FP8X4), scales=y_plane[:, tokens], in_=y_bf[:])
+            if c == CHUNKS - 2:
+                nc.sync.dma_start(codes_view[:, : S - CHUNK], y_codes[:, : S - CHUNK])
+
+        nc.sync.dma_start(codes_view[:, S - CHUNK :], y_codes[:, S - CHUNK :])
+        for q in range(4):
+            queue = nc.scalar if q % 2 == 0 else nc.sync
+            queue.dma_start(out_2[0, 4 * q : 4 * q + 4, :].bitcast(I32), y_plane[32 * q : 32 * q + 4, :].bitcast(I32))

@@ -19,6 +19,7 @@ P = 128
 PACK = 4
 CHUNK = 128
 CHUNKS = S // CHUNK
+WARM_PASSES = 6
 SCALAR_M = 24
 
 
@@ -30,54 +31,72 @@ def tile_picked_lora_gelu_po_kernel(
         keep = ctx.enter_context(tc.tile_pool(name="keep", bufs=1))
         psum = ctx.enter_context(tc.psum_pool(name="psum", bufs=1))
 
+        def sbuf(name, shape, dtype, tag=None):
+            return keep.tile(shape, dtype, name=name, tag=tag or name, align_bytes=64)
+
         offsets = keep.tile([P, S // 16], U16, name="offsets")
-        x_table = keep.tile([P, T], I32, name="x_table", align_bytes=64)
-        x_scale_table = keep.tile([P, T], U8, name="x_scale_table", align_bytes=64)
-        w2_rows = [keep.tile([P, 2, H], F32, name="w2_rows%d" % u, align_bytes=64) for u in range(2)]
-        w_words = keep.tile([P, 2, 2 * H], U8, name="w_words", align_bytes=64)
-        w_scales = keep.tile([P, 2, H], U8, name="w_scales", tag="w_scales", align_bytes=64)
-        warm = keep.tile([P, 2], F32, name="warm")
+        x_table = sbuf("x_table", [P, T], I32)
+        x_scale_table = sbuf("x_scale_table", [P, T], U8)
+        w2_rows = [sbuf("w2_rows%d" % u, [P, 2, H], F32) for u in range(2)]
+        w1_raw = sbuf("w1_raw", [P, 2 * H], U8)
+        w3_raw = sbuf("w3_raw", [P, 2 * H], U8)
+        w_scales = sbuf("w_scales", [P, 2, H], U8)
+        warm = sbuf("warm", [P, 2], F32)
 
         nc.vector.memset(x_scale_table[:].bitcast(I32), 0)
         nc.vector.memset(warm[:, 0:1], 0.0)
         nc.vector.memset(w_scales[:].rearrange("p w c -> p (w c)").bitcast(I32), 0)
 
-        def load_scales(queue, tile, scales, quadrants):
-            for q in quadrants:
-                queue.dma_start(tile[32 * q : 32 * q + 4, :].bitcast(I32), scales[0, 4 * q : 4 * q + 4, :].bitcast(I32))
+        def load_scales(tile, scales):
+            for q in range(4):
+                nc.sync.dma_start(tile[32 * q : 32 * q + 4, :].bitcast(I32), scales[0, 4 * q : 4 * q + 4, :].bitcast(I32))
 
         w2_view = w2.rearrange("(p j) c -> p j c", j=PACK)
-        nc.sync.dma_start(offsets[:], offs)
-        load_scales(nc.scalar, x_scale_table, x_scales, range(4))
         nc.scalar.activation(warm[:, 1:2], warm[:, 0:1], GELU)
-        nc.sync.dma_start(w_words[:, 0, :].bitcast(I32), w1_words[0].bitcast(I32))
-        nc.sync.dma_start(w_words[:, 1, :].bitcast(I32), w3_words[0].bitcast(I32))
-        for u in range(2):
-            nc.sync.dma_start(w2_rows[u][:], w2_view[:, 2 * u : 2 * u + 2, :])
+        nc.sync.dma_start(offsets[:], offs)
+        nc.sync.dma_start(w1_raw[:].bitcast(I32), w1_words[0].bitcast(I32))
+        nc.sync.dma_start(w3_raw[:].bitcast(I32), w3_words[0].bitcast(I32))
+        nc.sync.dma_start(w2_rows[0][:], w2_view[:, 0:2, :])
+        load_scales(x_scale_table, x_scales)
+        nc.sync.dma_start(w2_rows[1][:], w2_view[:, 2:4, :])
         nc.sync.dma_start(x_table[:], x_words[0].rearrange("p n r -> p (n r)").bitcast(I32))
-        load_scales(nc.gpsimd, w_scales[:, 0, :], w1_scales, range(2))
-        load_scales(nc.sync, w_scales[:, 0, :], w1_scales, range(2, 4))
-        load_scales(nc.sync, w_scales[:, 1, :], w3_scales, range(4))
+        load_scales(w_scales[:, 0, :], w1_scales)
+        load_scales(w_scales[:, 1, :], w3_scales)
 
-        dealt_words = keep.tile([P, PACK, 2, 2 * P], U8, name="dealt_words", align_bytes=64)
-        nc.vector.tensor_copy(
-            dealt_words[:].rearrange("p t w (g m b) -> p (w g) t m b", m=8, b=2),
-            w_words[:].rearrange("p w (g m t b) -> p (w g) t m b", m=8, t=PACK, b=2),
-        )
+        def deal_words(raw, name):
+            dealt = sbuf(name, [P, PACK, 2 * P], U8)
+            nc.vector.tensor_copy(
+                dealt[:].rearrange("p t (g m b) -> p g t m b", m=8, b=2),
+                raw[:].rearrange("p (g m t b) -> p g t m b", m=8, t=PACK, b=2),
+            )
+            return dealt
 
-        x_codes = keep.tile([P, S], U32, name="x_codes", align_bytes=64)
-        x_plane = keep.tile([P, S], U8, name="x_plane", align_bytes=64)
+        w1_dealt = deal_words(w1_raw, "w1_dealt")
+        w3_dealt = deal_words(w3_raw, "w3_dealt")
+
+        x_plane = sbuf("x_plane", [P, S], U8)
         nc.vector.tensor_copy(x_plane[:], x_scale_table[:].indirect(offsets[:]))
 
-        w2_bf = keep.tile([P, PACK * H], BF16, name="w2_bf", align_bytes=64)
+        def gather_words(c, tag):
+            codes = sbuf("x_codes%d" % c, [P, CHUNK], U32, tag)
+            nc.vector.tensor_copy(
+                codes[:], x_table[:].bitcast(U32).indirect(offsets[:, c * CHUNK // 16 : (c + 1) * CHUNK // 16])
+            )
+            return codes
+
+        w2_bf = sbuf("w2_bf", [P, PACK * H], BF16)
         w2_dst = w2_bf[:].rearrange("p (t g m j) -> p g t m j", t=PACK, m=2, j=PACK)
         srcs = [w2_rows[u][:].rearrange("p j (g m t) -> p g t m j", m=2, t=PACK) for u in range(2)]
         nc.scalar.copy(w2_dst[:, :, :, :, 0:2], srcs[0])
         cut = SCALAR_M // 2
         nc.scalar.copy(w2_dst[:, :cut, :, :, 2:4], srcs[1][:, :cut])
-        nc.vector.tensor_copy(w2_dst[:, cut:, :, :, 2:4], srcs[1][:, cut:])
-        w2_codes = keep.tile([P, H], U32, name="w2_codes", align_bytes=64)
-        w2_plane = keep.tile([P, H], U8, name="w2_plane", align_bytes=64)
+        for u in range(2):
+            nc.vector.tensor_copy(w2_dst[:, cut:, 2 * u : 2 * u + 2, :, 2:4], srcs[1][:, cut:, 2 * u : 2 * u + 2])
+
+        x_codes = [gather_words(0, None)]
+
+        w2_codes = sbuf("w2_codes", [P, H], U32)
+        w2_plane = sbuf("w2_plane", [P, H], U8)
         for t in range(PACK):
             cols = slice(t * P, (t + 1) * P)
             nc.vector.quantize_mx(
@@ -86,14 +105,19 @@ def tile_picked_lora_gelu_po_kernel(
                 in_=w2_bf[:, t * PACK * P : (t + 1) * PACK * P],
             )
 
-        for c in range(CHUNKS):
-            nc.vector.tensor_copy(
-                x_codes[:, c * CHUNK : (c + 1) * CHUNK],
-                x_table[:].bitcast(U32).indirect(offsets[:, c * CHUNK // 16 : (c + 1) * CHUNK // 16]),
+        idle = psum.tile([P, PACK, CHUNK], F32, name="idle", tag="acc3")
+        for i in range(WARM_PASSES):
+            nc.tensor.matmul_mx(
+                out=idle[:, i % PACK, :],
+                lhsT=w2_codes[:, :P].bitcast(FP8X4),
+                lhsT_scale=w2_plane[:, :P],
+                rhs=w2_codes[:, :CHUNK].bitcast(FP8X4),
+                rhs_scale=w2_plane[:, :CHUNK],
+                start=True,
+                stop=True,
             )
 
-        h_bf = []
-        for c in range(CHUNKS):
+        def hidden(c):
             tokens = slice(c * CHUNK, (c + 1) * CHUNK)
             pre = psum.tile([P, PACK, CHUNK], F32, name="pre%d" % c, tag="pre%d" % c)
             for t in range(PACK):
@@ -102,78 +126,85 @@ def tile_picked_lora_gelu_po_kernel(
                     out=pre[:, t, :],
                     lhsT=w2_codes[:, cols].bitcast(FP8X4),
                     lhsT_scale=w2_plane[:, cols],
-                    rhs=x_codes[:, tokens].bitcast(FP8X4),
+                    rhs=x_codes[c][:].bitcast(FP8X4),
                     rhs_scale=x_plane[:, tokens],
                     start=True,
                     stop=True,
                 )
-            hb = keep.tile([P, CHUNK * PACK], BF16, name="h_bf%d" % c, align_bytes=64)
-            nc.scalar.activation(hb[:].rearrange("p (n t) -> p n t", t=PACK), pre[:].rearrange("p t n -> p n t"), GELU)
-            h_bf.append(hb)
+            h_bf = sbuf("h_bf%d" % c, [P, CHUNK * PACK], BF16)
+            nc.scalar.activation(
+                h_bf[:].rearrange("p (n t) -> p n t", t=PACK), pre[:].rearrange("p t n -> p n t"), GELU
+            )
+            return h_bf
 
-        dealt_scales = keep.tile([P, PACK, 2, P], U8, name="dealt_scales", align_bytes=64)
+        def quantize_hidden(c):
+            tokens = slice(c * CHUNK, (c + 1) * CHUNK)
+            nc.vector.quantize_mx(out=h_codes[:, tokens].bitcast(FP8X4), scales=h_plane[:, tokens], in_=h_bf[c][:])
+
+        h_bf = [hidden(0)]
+        x_codes.append(gather_words(1, None))
+        h_bf.append(hidden(1))
+        x_codes.append(gather_words(2, None))
+        h_bf.append(hidden(2))
+
+        dealt_scales = sbuf("dealt_scales", [P, PACK, 2, P], U8)
         nc.vector.tensor_copy(
             dealt_scales[:].rearrange("p t w (g m) -> p (w g) t m", m=16),
             w_scales[:].rearrange("p w (g m t) -> p (w g) t m", m=16, t=PACK),
         )
+        h_codes = sbuf("h_codes", [P, S], U32)
+        h_plane = sbuf("h_plane", [P, S], U8, "w_scales")
+        quantize_hidden(0)
+        x_codes.append(gather_words(3, None))
+        h_bf.append(hidden(3))
+        for c in range(1, CHUNKS):
+            quantize_hidden(c)
 
-        y_codes = keep.tile([P, S], I32, name="y_codes", align_bytes=64)
-        y_plane = keep.tile([P, S], U8, name="y_plane", align_bytes=64)
+        y_codes = sbuf("y_codes", [P, S], I32)
+        y_plane = sbuf("y_plane", [P, S], U8)
         out_view = out_0.rearrange("(p t) j -> p t j", t=PACK)
         codes_view = out_1[0].rearrange("p n r -> p (n r)").bitcast(I32)
-
-        h_codes = keep.tile([P, S], U32, name="h_codes", align_bytes=64)
-        h_plane = keep.tile([P, S], U8, name="h_plane", tag="w_scales", align_bytes=64)
-        for c in range(CHUNKS):
-            tokens = slice(c * CHUNK, (c + 1) * CHUNK)
-            nc.vector.quantize_mx(out=h_codes[:, tokens].bitcast(FP8X4), scales=h_plane[:, tokens], in_=h_bf[c][:])
 
         for c in range(CHUNKS):
             tokens = slice(c * CHUNK, (c + 1) * CHUNK)
             last = c == CHUNKS - 1
-            if last:
-                low = psum.tile([P, 2, CHUNK], F32, name="low", tag="pre0")
-                high = psum.tile([P, 2, CHUNK], F32, name="high")
-                slots = [low[:, 0, :], low[:, 1, :], high[:, 0, :], high[:, 1, :]]
-            else:
-                acc = psum.tile([P, PACK, CHUNK], F32, name="acc%d" % c)
-                slots = [acc[:, t, :] for t in range(PACK)]
+            banks = [
+                psum.tile([P, 2, CHUNK], F32, name="acc%d_%d" % (c, u), tag=("acc%d" if c < 2 else "pre%d") % (c % 2 * 2 + u))
+                for u in range(2)
+            ]
             for t in range(PACK):
-                nc.tensor.matmul_mx(
-                    out=slots[t],
-                    lhsT=dealt_words[:, t, 0, :].bitcast(FP4X4),
-                    lhsT_scale=dealt_scales[:, t, 0, :],
-                    rhs=x_codes[:, tokens].bitcast(FP8X4),
-                    rhs_scale=x_plane[:, tokens],
-                    start=True,
-                    stop=False,
-                )
-                nc.tensor.matmul_mx(
-                    out=slots[t],
-                    lhsT=dealt_words[:, t, 1, :].bitcast(FP4X4),
-                    lhsT_scale=dealt_scales[:, t, 1, :],
-                    rhs=h_codes[:, tokens].bitcast(FP8X4),
-                    rhs_scale=h_plane[:, tokens],
-                    start=False,
-                    stop=True,
-                )
-            y = keep.tile([P, PACK, CHUNK], F32, name="y%d" % c, align_bytes=64)
+                for w, dealt, codes, plane in (
+                    (0, w1_dealt, x_codes[c][:], x_plane),
+                    (1, w3_dealt, h_codes[:, tokens], h_plane),
+                ):
+                    nc.tensor.matmul_mx(
+                        out=banks[t // 2][:, t % 2, :],
+                        lhsT=dealt[:, t, :].bitcast(FP4X4),
+                        lhsT_scale=dealt_scales[:, t, w, :],
+                        rhs=codes.bitcast(FP8X4),
+                        rhs_scale=plane[:, tokens],
+                        start=w == 0,
+                        stop=w == 1,
+                    )
+            y = sbuf("y%d" % c, [P, PACK, CHUNK], F32)
+            y_bf = sbuf("y_bf%d" % c, [P, CHUNK * PACK], BF16)
+            dst = y_bf[:].rearrange("p (g i t) -> p g t i", i=4, t=PACK)
+            src = y[:].rearrange("p t (g i) -> p g t i", i=4)
+            for u in range(2):
+                nc.scalar.copy(y[:, 2 * u : 2 * u + 2, :], banks[u][:])
             if last:
-                nc.scalar.copy(y[:, 0:2, :], low[:])
-                nc.vector.tensor_copy(y[:, 2:4, :], high[:])
+                nc.vector.tensor_copy(dst[:, :, 0:2], src[:, :, 0:2])
+                nc.scalar.copy(
+                    y_bf[:].rearrange("p (n t) -> p n t", t=PACK)[:, :, 2:4], banks[1][:].rearrange("p t n -> p n t")
+                )
             else:
-                nc.scalar.copy(y[:], acc[:])
+                nc.vector.tensor_copy(dst, src)
             nc.sync.dma_start(out_view[:, :, tokens], y[:])
-            y_bf = keep.tile([P, CHUNK * PACK], BF16, name="y_bf%d" % c, align_bytes=64)
-            nc.vector.tensor_copy(
-                y_bf[:].rearrange("p (g i t) -> p g t i", i=4, t=PACK),
-                y[:].rearrange("p t (g i) -> p g t i", i=4),
-            )
             nc.vector.quantize_mx(out=y_codes[:, tokens].bitcast(FP8X4), scales=y_plane[:, tokens], in_=y_bf[:])
-            if c == CHUNKS - 2:
-                nc.sync.dma_start(codes_view[:, : S - CHUNK], y_codes[:, : S - CHUNK])
+            if c % 2 == 1:
+                pair = slice((c - 1) * CHUNK, (c + 1) * CHUNK)
+                nc.sync.dma_start(codes_view[:, pair], y_codes[:, pair])
 
-        nc.sync.dma_start(codes_view[:, S - CHUNK :], y_codes[:, S - CHUNK :])
         for q in range(4):
             queue = nc.scalar if q % 2 == 0 else nc.sync
             queue.dma_start(out_2[0, 4 * q : 4 * q + 4, :].bitcast(I32), y_plane[32 * q : 32 * q + 4, :].bitcast(I32))

@@ -20,7 +20,6 @@ PACK = 4
 CHUNK = 128
 CHUNKS = S // CHUNK
 WARM_PASSES = 6
-SCALAR_M = 24
 
 
 def tile_picked_lora_gelu_po_kernel(
@@ -41,10 +40,8 @@ def tile_picked_lora_gelu_po_kernel(
         w1_raw = sbuf("w1_raw", [P, 2 * H], U8)
         w3_raw = sbuf("w3_raw", [P, 2 * H], U8)
         w_scales = sbuf("w_scales", [P, 2, H], U8)
-        warm = sbuf("warm", [P, 2], F32)
 
         nc.vector.memset(x_scale_table[:].bitcast(I32), 0)
-        nc.vector.memset(warm[:, 0:1], 0.0)
         nc.vector.memset(w_scales[:].rearrange("p w c -> p (w c)").bitcast(I32), 0)
 
         def load_scales(tile, scales):
@@ -52,7 +49,6 @@ def tile_picked_lora_gelu_po_kernel(
                 nc.sync.dma_start(tile[32 * q : 32 * q + 4, :].bitcast(I32), scales[0, 4 * q : 4 * q + 4, :].bitcast(I32))
 
         w2_view = w2.rearrange("(p j) c -> p j c", j=PACK)
-        nc.scalar.activation(warm[:, 1:2], warm[:, 0:1], GELU)
         nc.sync.dma_start(offsets[:], offs)
         nc.sync.dma_start(w1_raw[:].bitcast(I32), w1_words[0].bitcast(I32))
         nc.sync.dma_start(w3_raw[:].bitcast(I32), w3_words[0].bitcast(I32))
@@ -88,10 +84,8 @@ def tile_picked_lora_gelu_po_kernel(
         w2_dst = w2_bf[:].rearrange("p (t g m j) -> p g t m j", t=PACK, m=2, j=PACK)
         srcs = [w2_rows[u][:].rearrange("p j (g m t) -> p g t m j", m=2, t=PACK) for u in range(2)]
         nc.scalar.copy(w2_dst[:, :, :, :, 0:2], srcs[0])
-        cut = SCALAR_M // 2
-        nc.scalar.copy(w2_dst[:, :cut, :, :, 2:4], srcs[1][:, :cut])
         for u in range(2):
-            nc.vector.tensor_copy(w2_dst[:, cut:, 2 * u : 2 * u + 2, :, 2:4], srcs[1][:, cut:, 2 * u : 2 * u + 2])
+            nc.vector.tensor_copy(w2_dst[:, :, 2 * u : 2 * u + 2, :, 2:4], srcs[1][:, :, 2 * u : 2 * u + 2])
 
         x_codes = [gather_words(0, None)]
 
@@ -186,12 +180,15 @@ def tile_picked_lora_gelu_po_kernel(
                         start=w == 0,
                         stop=w == 1,
                     )
-            y = sbuf("y%d" % c, [P, PACK, CHUNK], F32)
+            if c % 2 == 0:
+                y_pair = sbuf("y%d" % c, [P, PACK, 2 * CHUNK], F32)
+            y = y_pair[:, :, c % 2 * CHUNK : (c % 2 + 1) * CHUNK]
             y_bf = sbuf("y_bf%d" % c, [P, CHUNK * PACK], BF16)
             dst = y_bf[:].rearrange("p (g i t) -> p g t i", i=4, t=PACK)
-            src = y[:].rearrange("p t (g i) -> p g t i", i=4)
+            src = y.rearrange("p t (g i) -> p g t i", i=4)
             for u in range(2):
-                nc.scalar.copy(y[:, 2 * u : 2 * u + 2, :], banks[u][:])
+                copy = nc.vector.tensor_copy if (c, u) == (1, 0) else nc.scalar.copy
+                copy(y[:, 2 * u : 2 * u + 2, :], banks[u][:])
             if last:
                 nc.vector.tensor_copy(dst[:, :, 0:2], src[:, :, 0:2])
                 nc.scalar.copy(
@@ -199,7 +196,10 @@ def tile_picked_lora_gelu_po_kernel(
                 )
             else:
                 nc.vector.tensor_copy(dst, src)
-            nc.sync.dma_start(out_view[:, :, tokens], y[:])
+            if c < 2:
+                nc.sync.dma_start(out_view[:, :, tokens], y)
+            elif last:
+                nc.sync.dma_start(out_view[:, :, S // 2 :], y_pair[:])
             nc.vector.quantize_mx(out=y_codes[:, tokens].bitcast(FP8X4), scales=y_plane[:, tokens], in_=y_bf[:])
             if c % 2 == 1:
                 pair = slice((c - 1) * CHUNK, (c + 1) * CHUNK)

@@ -19,7 +19,6 @@ P = 128
 PACK = 4
 CHUNK = 128
 CHUNKS = S // CHUNK
-WARM_PASSES = 6
 
 
 def tile_picked_lora_gelu_po_kernel(
@@ -36,80 +35,107 @@ def tile_picked_lora_gelu_po_kernel(
         offsets = keep.tile([P, S // 16], U16, name="offsets")
         x_table = sbuf("x_table", [P, T], I32)
         x_scale_table = sbuf("x_scale_table", [P, T], U8)
-        w2_rows = [sbuf("w2_rows%d" % u, [P, 2, H], F32) for u in range(2)]
+        w2_cols = [sbuf("w2_cols%d" % u, [P, PACK, H // 2], F32) for u in range(2)]
         w1_raw = sbuf("w1_raw", [P, 2 * H], U8)
         w3_raw = sbuf("w3_raw", [P, 2 * H], U8)
-        w_scales = sbuf("w_scales", [P, 2, H], U8)
+        w_scales = sbuf("w_scales", [P, 2 * H], U8)
 
         nc.vector.memset(x_scale_table[:].bitcast(I32), 0)
-        nc.vector.memset(w_scales[:].rearrange("p w c -> p (w c)").bitcast(I32), 0)
+        nc.gpsimd.memset(w_scales[:].bitcast(I32), 0)
 
-        def load_scales(tile, scales):
-            for q in range(4):
-                nc.sync.dma_start(tile[32 * q : 32 * q + 4, :].bitcast(I32), scales[0, 4 * q : 4 * q + 4, :].bitcast(I32))
+        seed = sbuf("seed", [P, 2], F32)
+        nc.gpsimd.memset(seed[:, 0:1], 0.0)
+        nc.scalar.activation(seed[:, 1:2], seed[:, 0:1], GELU)
+
+        def load_weight_scales(queue, w, q):
+            rows = w_scales[32 * q : 32 * q + 4, :].bitcast(I32).rearrange("p (u w c) -> p u w c", u=2, w=2)
+            scales = (w1_scales, w3_scales)[w]
+            queue.dma_start(rows[:, :, w, :], scales[0, 4 * q : 4 * q + 4, :].bitcast(I32).rearrange("p (u c) -> p u c", u=2))
 
         w2_view = w2.rearrange("(p j) c -> p j c", j=PACK)
+        weight_rows = [(w, q) for w in range(2) for q in range(4)]
+        for w, q in weight_rows[:2]:
+            load_weight_scales(nc.gpsimd, w, q)
         nc.sync.dma_start(offsets[:], offs)
         nc.sync.dma_start(w1_raw[:].bitcast(I32), w1_words[0].bitcast(I32))
-        nc.sync.dma_start(w3_raw[:].bitcast(I32), w3_words[0].bitcast(I32))
-        nc.sync.dma_start(w2_rows[0][:], w2_view[:, 0:2, :])
-        load_scales(x_scale_table, x_scales)
-        nc.sync.dma_start(w2_rows[1][:], w2_view[:, 2:4, :])
+        nc.sync.dma_start(w2_cols[0][:], w2_view[:, :, : H // 2])
+        for q in range(4):
+            nc.sync.dma_start(
+                x_scale_table[32 * q : 32 * q + 4, :].bitcast(I32), x_scales[0, 4 * q : 4 * q + 4, :].bitcast(I32)
+            )
+        nc.sync.dma_start(w2_cols[1][:], w2_view[:, :, H // 2 :])
         nc.sync.dma_start(x_table[:], x_words[0].rearrange("p n r -> p (n r)").bitcast(I32))
-        load_scales(w_scales[:, 0, :], w1_scales)
-        load_scales(w_scales[:, 1, :], w3_scales)
+        nc.sync.dma_start(w3_raw[:].bitcast(I32), w3_words[0].bitcast(I32))
+        for w, q in weight_rows[2:]:
+            load_weight_scales(nc.sync, w, q)
 
         def deal_words(raw, name):
             dealt = sbuf(name, [P, PACK, 2 * P], U8)
             nc.vector.tensor_copy(
-                dealt[:].rearrange("p t (g m b) -> p g t m b", m=8, b=2),
-                raw[:].rearrange("p (g m t b) -> p g t m b", m=8, t=PACK, b=2),
+                dealt[:].bitcast(U16).rearrange("p t (g m) -> p g t m", m=8),
+                raw[:].bitcast(U16).rearrange("p (g m t) -> p g t m", m=8, t=PACK),
             )
             return dealt
 
-        w1_dealt = deal_words(w1_raw, "w1_dealt")
-        w3_dealt = deal_words(w3_raw, "w3_dealt")
-
-        x_plane = sbuf("x_plane", [P, S], U8)
-        nc.vector.tensor_copy(x_plane[:], x_scale_table[:].indirect(offsets[:]))
-
-        def gather_words(c, tag):
-            codes = sbuf("x_codes%d" % c, [P, CHUNK], U32, tag)
+        def gather_words(c):
+            codes = sbuf("x_codes%d" % c, [P, CHUNK], U32)
             nc.vector.tensor_copy(
                 codes[:], x_table[:].bitcast(U32).indirect(offsets[:, c * CHUNK // 16 : (c + 1) * CHUNK // 16])
             )
             return codes
 
-        w2_bf = sbuf("w2_bf", [P, PACK * H], BF16)
-        w2_dst = w2_bf[:].rearrange("p (t g m j) -> p g t m j", t=PACK, m=2, j=PACK)
-        srcs = [w2_rows[u][:].rearrange("p j (g m t) -> p g t m j", m=2, t=PACK) for u in range(2)]
-        nc.scalar.copy(w2_dst[:, :, :, :, 0:2], srcs[0])
-        for u in range(2):
-            nc.vector.tensor_copy(w2_dst[:, :, 2 * u : 2 * u + 2, :, 2:4], srcs[1][:, :, 2 * u : 2 * u + 2])
-
-        x_codes = [gather_words(0, None)]
+        w1_dealt = deal_words(w1_raw, "w1_dealt")
+        x_plane = sbuf("x_plane", [P, S], U8)
+        nc.vector.tensor_copy(x_plane[:], x_scale_table[:].indirect(offsets[:]))
 
         w2_codes = sbuf("w2_codes", [P, H], U32)
-        w2_plane = sbuf("w2_plane", [P, H], U8)
-        for t in range(PACK):
-            cols = slice(t * P, (t + 1) * P)
-            nc.vector.quantize_mx(
-                out=w2_codes[:, cols].bitcast(FP8X4),
-                scales=w2_plane[:, cols],
-                in_=w2_bf[:, t * PACK * P : (t + 1) * PACK * P],
+        w2_plane = sbuf("w2_plane", [P, H], U8, "x_scale_table")
+        for u in range(2):
+            w2_bf = sbuf("w2_bf%d" % u, [P, PACK * H // 2], BF16)
+            nc.scalar.copy(
+                w2_bf[:].rearrange("p (t m j) -> p m j t", t=PACK, j=PACK),
+                w2_cols[u][:].rearrange("p j (m t) -> p m j t", t=PACK),
+            )
+            if u == 1:
+                x_codes = [gather_words(0)]
+            for t in range(PACK):
+                first = t * P + u * P // 2
+                nc.vector.quantize_mx(
+                    out=w2_codes[:, first : first + P // 2].bitcast(FP8X4),
+                    scales=w2_plane[:, first : first + P // 2],
+                    in_=w2_bf[:, t * H // 2 : (t + 1) * H // 2],
+                )
+
+        x_codes.extend(gather_words(c) for c in range(1, CHUNKS))
+
+        def product(out, dealt, w, t, codes, plane, c, start, stop):
+            tokens = slice(c * CHUNK, (c + 1) * CHUNK)
+            nc.tensor.matmul_mx(
+                out=out,
+                lhsT=dealt[:, t, :].bitcast(FP4X4),
+                lhsT_scale=w_plane[:, w, t, :],
+                rhs=codes.bitcast(FP8X4),
+                rhs_scale=plane[:, tokens],
+                start=start,
+                stop=stop,
             )
 
-        idle = psum.tile([P, PACK, CHUNK], F32, name="idle", tag="acc3")
-        for i in range(WARM_PASSES):
-            nc.tensor.matmul_mx(
-                out=idle[:, i % PACK, :],
-                lhsT=w2_codes[:, :P].bitcast(FP8X4),
-                lhsT_scale=w2_plane[:, :P],
-                rhs=w2_codes[:, :CHUNK].bitcast(FP8X4),
-                rhs_scale=w2_plane[:, :CHUNK],
-                start=True,
-                stop=True,
-            )
+        def open_sums(c):
+            tags = ["acc%d" % c] if c < CHUNKS - 1 else ["acc%d" % c, "pre0"]
+            per_bank = PACK // len(tags)
+            banks = [psum.tile([P, per_bank, CHUNK], F32, name="acc%d_%d" % (c, u), tag=tag) for u, tag in enumerate(tags)]
+            for t in range(PACK):
+                product(banks[t // per_bank][:, t % per_bank, :], w1_dealt, 0, t, x_codes[c][:], x_plane, c, t % per_bank == 0, False)
+            return banks
+
+        def close_sums(c):
+            banks = sums[c]
+            per_bank = PACK // len(banks)
+            for t in range(PACK):
+                product(
+                    banks[t // per_bank][:, t % per_bank, :], w3_dealt, 1, t, h_codes[:, c * CHUNK : (c + 1) * CHUNK], h_plane, c, False,
+                    t % per_bank == per_bank - 1,
+                )
 
         def hidden(c):
             tokens = slice(c * CHUNK, (c + 1) * CHUNK)
@@ -131,28 +157,23 @@ def tile_picked_lora_gelu_po_kernel(
             )
             return h_bf
 
-        def quantize_hidden(c):
+        h_bf = [hidden(c) for c in range(CHUNKS)]
+        w3_dealt = deal_words(w3_raw, "w3_dealt")
+        w_plane = sbuf("w_plane", [P, 2, PACK, P], U8)
+        for u in range(2):
+            nc.vector.tensor_copy(
+                w_plane[:, :, :, u * P // 2 : (u + 1) * P // 2].rearrange("p w t (g m) -> p w g t m", m=16),
+                w_scales[:, u * H : (u + 1) * H].rearrange("p (w g m t) -> p w g t m", w=2, m=16, t=PACK),
+            )
+
+        h_codes = sbuf("h_codes", [P, S], U32)
+        h_plane = w_scales[:, :S]
+        sums = []
+        for c in range(CHUNKS):
             tokens = slice(c * CHUNK, (c + 1) * CHUNK)
             nc.vector.quantize_mx(out=h_codes[:, tokens].bitcast(FP8X4), scales=h_plane[:, tokens], in_=h_bf[c][:])
-
-        h_bf = [hidden(0)]
-        x_codes.append(gather_words(1, None))
-        h_bf.append(hidden(1))
-        x_codes.append(gather_words(2, None))
-        h_bf.append(hidden(2))
-
-        dealt_scales = sbuf("dealt_scales", [P, PACK, 2, P], U8)
-        nc.vector.tensor_copy(
-            dealt_scales[:].rearrange("p t w (g m) -> p (w g) t m", m=16),
-            w_scales[:].rearrange("p w (g m t) -> p (w g) t m", m=16, t=PACK),
-        )
-        h_codes = sbuf("h_codes", [P, S], U32)
-        h_plane = sbuf("h_plane", [P, S], U8, "w_scales")
-        quantize_hidden(0)
-        x_codes.append(gather_words(3, None))
-        h_bf.append(hidden(3))
-        for c in range(1, CHUNKS):
-            quantize_hidden(c)
+            sums.append(open_sums(c))
+            close_sums(c)
 
         y_codes = sbuf("y_codes", [P, S], I32)
         y_plane = sbuf("y_plane", [P, S], U8)
@@ -162,49 +183,26 @@ def tile_picked_lora_gelu_po_kernel(
         for c in range(CHUNKS):
             tokens = slice(c * CHUNK, (c + 1) * CHUNK)
             last = c == CHUNKS - 1
-            banks = [
-                psum.tile([P, 2, CHUNK], F32, name="acc%d_%d" % (c, u), tag=("acc%d" if c < 2 else "pre%d") % (c % 2 * 2 + u))
-                for u in range(2)
-            ]
-            for t in range(PACK):
-                for w, dealt, codes, plane in (
-                    (0, w1_dealt, x_codes[c][:], x_plane),
-                    (1, w3_dealt, h_codes[:, tokens], h_plane),
-                ):
-                    nc.tensor.matmul_mx(
-                        out=banks[t // 2][:, t % 2, :],
-                        lhsT=dealt[:, t, :].bitcast(FP4X4),
-                        lhsT_scale=dealt_scales[:, t, w, :],
-                        rhs=codes.bitcast(FP8X4),
-                        rhs_scale=plane[:, tokens],
-                        start=w == 0,
-                        stop=w == 1,
-                    )
-            if c % 2 == 0:
-                y_pair = sbuf("y%d" % c, [P, PACK, 2 * CHUNK], F32)
-            y = y_pair[:, :, c % 2 * CHUNK : (c % 2 + 1) * CHUNK]
+            banks = sums[c]
+            y_tile = sbuf("y%d" % c, [P, PACK, CHUNK], F32)
+            y = y_tile[:]
             y_bf = sbuf("y_bf%d" % c, [P, CHUNK * PACK], BF16)
             dst = y_bf[:].rearrange("p (g i t) -> p g t i", i=4, t=PACK)
             src = y.rearrange("p t (g i) -> p g t i", i=4)
-            for u in range(2):
-                copy = nc.vector.tensor_copy if (c, u) == (1, 0) else nc.scalar.copy
-                copy(y[:, 2 * u : 2 * u + 2, :], banks[u][:])
             if last:
+                for u in range(2):
+                    nc.scalar.copy(y[:, 2 * u : 2 * u + 2, :], banks[u][:])
                 nc.vector.tensor_copy(dst[:, :, 0:2], src[:, :, 0:2])
                 nc.scalar.copy(
                     y_bf[:].rearrange("p (n t) -> p n t", t=PACK)[:, :, 2:4], banks[1][:].rearrange("p t n -> p n t")
                 )
             else:
+                nc.scalar.copy(y, banks[0][:])
                 nc.vector.tensor_copy(dst, src)
-            if c < 2:
-                nc.sync.dma_start(out_view[:, :, tokens], y)
-            elif last:
-                nc.sync.dma_start(out_view[:, :, S // 2 :], y_pair[:])
+            nc.sync.dma_start(out_view[:, :, tokens], y)
             nc.vector.quantize_mx(out=y_codes[:, tokens].bitcast(FP8X4), scales=y_plane[:, tokens], in_=y_bf[:])
-            if c % 2 == 1:
-                pair = slice((c - 1) * CHUNK, (c + 1) * CHUNK)
-                nc.sync.dma_start(codes_view[:, pair], y_codes[:, pair])
 
+        nc.sync.dma_start(codes_view, y_codes[:])
         for q in range(4):
             queue = nc.scalar if q % 2 == 0 else nc.sync
             queue.dma_start(out_2[0, 4 * q : 4 * q + 4, :].bitcast(I32), y_plane[32 * q : 32 * q + 4, :].bitcast(I32))

@@ -180,29 +180,47 @@ def tile_picked_lora_gelu_po_kernel(
         out_view = out_0.rearrange("(p t) j -> p t j", t=PACK)
         codes_view = out_1[0].rearrange("p n r -> p (n r)").bitcast(I32)
 
+        y_bf = [sbuf("y_bf%d" % u, [P, count * CHUNK * PACK], BF16) for u, count in enumerate((2, 1, 1))]
+        rounded_chunks = [y_bf[0][:, : CHUNK * PACK], y_bf[0][:, CHUNK * PACK :], y_bf[1][:], y_bf[2][:]]
+
+        def quantize_result(first, count, values):
+            tokens = slice(first * CHUNK, (first + count) * CHUNK)
+            nc.vector.quantize_mx(
+                out=y_codes[:, tokens].bitcast(FP8X4),
+                scales=y_plane[:, tokens],
+                in_=values[:],
+            )
+
         for c in range(CHUNKS):
             tokens = slice(c * CHUNK, (c + 1) * CHUNK)
-            last = c == CHUNKS - 1
             banks = sums[c]
-            y_tile = sbuf("y%d" % c, [P, PACK, CHUNK], F32)
-            y = y_tile[:]
-            y_bf = sbuf("y_bf%d" % c, [P, CHUNK * PACK], BF16)
-            dst = y_bf[:].rearrange("p (g i t) -> p g t i", i=4, t=PACK)
+            if c % 2 == 0:
+                y_pair = sbuf("y%d" % c, [P, PACK, 2 * CHUNK], F32)
+            y = y_pair[:, :, c % 2 * CHUNK : (c % 2 + 1) * CHUNK]
+            rounded = rounded_chunks[c]
+            dst = rounded.rearrange("p (g i t) -> p g t i", i=4, t=PACK)
             src = y.rearrange("p t (g i) -> p g t i", i=4)
-            if last:
+            if c == CHUNKS - 1:
                 for u in range(2):
                     nc.scalar.copy(y[:, 2 * u : 2 * u + 2, :], banks[u][:])
                 nc.vector.tensor_copy(dst[:, :, 0:2], src[:, :, 0:2])
                 nc.scalar.copy(
-                    y_bf[:].rearrange("p (n t) -> p n t", t=PACK)[:, :, 2:4], banks[1][:].rearrange("p t n -> p n t")
+                    rounded.rearrange("p (n t) -> p n t", t=PACK)[:, :, 2:4], banks[1][:].rearrange("p t n -> p n t")
                 )
             else:
                 nc.scalar.copy(y, banks[0][:])
                 nc.vector.tensor_copy(dst, src)
-            nc.sync.dma_start(out_view[:, :, tokens], y)
-            nc.vector.quantize_mx(out=y_codes[:, tokens].bitcast(FP8X4), scales=y_plane[:, tokens], in_=y_bf[:])
+            if c < 2:
+                nc.sync.dma_start(out_view[:, :, tokens], y)
+            elif c == CHUNKS - 1:
+                nc.sync.dma_start(out_view[:, :, S // 2 :], y_pair[:])
+            if c == 1:
+                quantize_result(0, 2, y_bf[0])
+                nc.sync.dma_start(codes_view[:, : S // 2], y_codes[:, : S // 2])
+        quantize_result(2, 1, y_bf[1])
+        quantize_result(3, 1, y_bf[2])
 
-        nc.sync.dma_start(codes_view, y_codes[:])
+        nc.sync.dma_start(codes_view[:, S // 2 :], y_codes[:, S // 2 :])
         for q in range(4):
             queue = nc.scalar if q % 2 == 0 else nc.sync
             queue.dma_start(out_2[0, 4 * q : 4 * q + 4, :].bitcast(I32), y_plane[32 * q : 32 * q + 4, :].bitcast(I32))

@@ -36,8 +36,7 @@ def tile_picked_lora_gelu_po_kernel(
         x_table = sbuf("x_table", [P, T], I32)
         x_scale_table = sbuf("x_scale_table", [P, T], U8)
         w2_cols = [sbuf("w2_cols%d" % u, [P, PACK, H // 2], F32) for u in range(2)]
-        w1_raw = sbuf("w1_raw", [P, 2 * H], U8)
-        w3_raw = sbuf("w3_raw", [P, 2 * H], U8)
+        w_raw = sbuf("w_raw", [P, 2, 2 * H], U8)
         w_scales = sbuf("w_scales", [P, 2 * H], U8)
 
         nc.vector.memset(x_scale_table[:].bitcast(I32), 0)
@@ -54,37 +53,29 @@ def tile_picked_lora_gelu_po_kernel(
 
         w2_view = w2.rearrange("(p j) c -> p j c", j=PACK)
         weight_rows = [(w, q) for w in range(2) for q in range(4)]
-        for w, q in weight_rows[:2]:
+        for w, q in weight_rows[:3]:
             load_weight_scales(nc.gpsimd, w, q)
-        nc.sync.dma_start(offsets[:], offs)
-        nc.sync.dma_start(w1_raw[:].bitcast(I32), w1_words[0].bitcast(I32))
         nc.sync.dma_start(w2_cols[0][:], w2_view[:, :, : H // 2])
+        nc.sync.dma_start(offsets[:], offs)
         for q in range(4):
             nc.sync.dma_start(
                 x_scale_table[32 * q : 32 * q + 4, :].bitcast(I32), x_scales[0, 4 * q : 4 * q + 4, :].bitcast(I32)
             )
         nc.sync.dma_start(w2_cols[1][:], w2_view[:, :, H // 2 :])
         nc.sync.dma_start(x_table[:], x_words[0].rearrange("p n r -> p (n r)").bitcast(I32))
-        nc.sync.dma_start(w3_raw[:].bitcast(I32), w3_words[0].bitcast(I32))
-        for w, q in weight_rows[2:]:
+        nc.sync.dma_start(w_raw[:, 0, :].bitcast(I32), w1_words[0].bitcast(I32))
+        nc.sync.dma_start(w_raw[:, 1, :].bitcast(I32), w3_words[0].bitcast(I32))
+        for w, q in weight_rows[3:]:
             load_weight_scales(nc.sync, w, q)
 
-        def deal_words(raw, name):
-            dealt = sbuf(name, [P, PACK, 2 * P], U8)
+        def gather_words(first, count):
+            codes = sbuf("x_codes%d" % first, [P, count * CHUNK], U32)
             nc.vector.tensor_copy(
-                dealt[:].bitcast(U16).rearrange("p t (g m) -> p g t m", m=8),
-                raw[:].bitcast(U16).rearrange("p (g m t) -> p g t m", m=8, t=PACK),
+                codes[:],
+                x_table[:].bitcast(U32).indirect(offsets[:, first * CHUNK // 16 : (first + count) * CHUNK // 16]),
             )
-            return dealt
+            return [codes[:, c * CHUNK : (c + 1) * CHUNK] for c in range(count)]
 
-        def gather_words(c):
-            codes = sbuf("x_codes%d" % c, [P, CHUNK], U32)
-            nc.vector.tensor_copy(
-                codes[:], x_table[:].bitcast(U32).indirect(offsets[:, c * CHUNK // 16 : (c + 1) * CHUNK // 16])
-            )
-            return codes
-
-        w1_dealt = deal_words(w1_raw, "w1_dealt")
         x_plane = sbuf("x_plane", [P, S], U8)
         nc.vector.tensor_copy(x_plane[:], x_scale_table[:].indirect(offsets[:]))
 
@@ -97,7 +88,7 @@ def tile_picked_lora_gelu_po_kernel(
                 w2_cols[u][:].rearrange("p j (m t) -> p m j t", t=PACK),
             )
             if u == 1:
-                x_codes = [gather_words(0)]
+                x_codes = gather_words(0, 1)
             for t in range(PACK):
                 first = t * P + u * P // 2
                 nc.vector.quantize_mx(
@@ -106,13 +97,13 @@ def tile_picked_lora_gelu_po_kernel(
                     in_=w2_bf[:, t * H // 2 : (t + 1) * H // 2],
                 )
 
-        x_codes.extend(gather_words(c) for c in range(1, CHUNKS))
+        x_codes = x_codes + gather_words(1, 1) + gather_words(2, 2)
 
-        def product(out, dealt, w, t, codes, plane, c, start, stop):
+        def product(out, w, t, codes, plane, c, start, stop):
             tokens = slice(c * CHUNK, (c + 1) * CHUNK)
             nc.tensor.matmul_mx(
                 out=out,
-                lhsT=dealt[:, t, :].bitcast(FP4X4),
+                lhsT=w_dealt[:, w, t, :].bitcast(FP4X4),
                 lhsT_scale=w_plane[:, w, t, :],
                 rhs=codes.bitcast(FP8X4),
                 rhs_scale=plane[:, tokens],
@@ -125,7 +116,7 @@ def tile_picked_lora_gelu_po_kernel(
             per_bank = PACK // len(tags)
             banks = [psum.tile([P, per_bank, CHUNK], F32, name="acc%d_%d" % (c, u), tag=tag) for u, tag in enumerate(tags)]
             for t in range(PACK):
-                product(banks[t // per_bank][:, t % per_bank, :], w1_dealt, 0, t, x_codes[c][:], x_plane, c, t % per_bank == 0, False)
+                product(banks[t // per_bank][:, t % per_bank, :], 0, t, x_codes[c], x_plane, c, t % per_bank == 0, False)
             return banks
 
         def close_sums(c):
@@ -133,7 +124,7 @@ def tile_picked_lora_gelu_po_kernel(
             per_bank = PACK // len(banks)
             for t in range(PACK):
                 product(
-                    banks[t // per_bank][:, t % per_bank, :], w3_dealt, 1, t, h_codes[:, c * CHUNK : (c + 1) * CHUNK], h_plane, c, False,
+                    banks[t // per_bank][:, t % per_bank, :], 1, t, h_codes[:, c * CHUNK : (c + 1) * CHUNK], h_plane, c, False,
                     t % per_bank == per_bank - 1,
                 )
 
@@ -146,7 +137,7 @@ def tile_picked_lora_gelu_po_kernel(
                     out=pre[:, t, :],
                     lhsT=w2_codes[:, cols].bitcast(FP8X4),
                     lhsT_scale=w2_plane[:, cols],
-                    rhs=x_codes[c][:].bitcast(FP8X4),
+                    rhs=x_codes[c].bitcast(FP8X4),
                     rhs_scale=x_plane[:, tokens],
                     start=True,
                     stop=True,
@@ -158,7 +149,11 @@ def tile_picked_lora_gelu_po_kernel(
             return h_bf
 
         h_bf = [hidden(c) for c in range(CHUNKS)]
-        w3_dealt = deal_words(w3_raw, "w3_dealt")
+        w_dealt = sbuf("w_dealt", [P, 2, PACK, 2 * P], U8)
+        nc.vector.tensor_copy(
+            w_dealt[:].bitcast(U16).rearrange("p w t (g m) -> p w g t m", m=8),
+            w_raw[:].bitcast(U16).rearrange("p w (g m t) -> p w g t m", m=8, t=PACK),
+        )
         w_plane = sbuf("w_plane", [P, 2, PACK, P], U8)
         for u in range(2):
             nc.vector.tensor_copy(
@@ -194,9 +189,8 @@ def tile_picked_lora_gelu_po_kernel(
         for c in range(CHUNKS):
             tokens = slice(c * CHUNK, (c + 1) * CHUNK)
             banks = sums[c]
-            if c % 2 == 0:
-                y_pair = sbuf("y%d" % c, [P, PACK, 2 * CHUNK], F32)
-            y = y_pair[:, :, c % 2 * CHUNK : (c % 2 + 1) * CHUNK]
+            y_tile = sbuf("y%d" % c, [P, PACK, CHUNK], F32)
+            y = y_tile[:]
             rounded = rounded_chunks[c]
             dst = rounded.rearrange("p (g i t) -> p g t i", i=4, t=PACK)
             src = y.rearrange("p t (g i) -> p g t i", i=4)
@@ -210,17 +204,13 @@ def tile_picked_lora_gelu_po_kernel(
             else:
                 nc.scalar.copy(y, banks[0][:])
                 nc.vector.tensor_copy(dst, src)
-            if c < 2:
-                nc.sync.dma_start(out_view[:, :, tokens], y)
-            elif c == CHUNKS - 1:
-                nc.sync.dma_start(out_view[:, :, S // 2 :], y_pair[:])
+            nc.sync.dma_start(out_view[:, :, tokens], y)
             if c == 1:
                 quantize_result(0, 2, y_bf[0])
-                nc.sync.dma_start(codes_view[:, : S // 2], y_codes[:, : S // 2])
         quantize_result(2, 1, y_bf[1])
         quantize_result(3, 1, y_bf[2])
 
-        nc.sync.dma_start(codes_view[:, S // 2 :], y_codes[:, S // 2 :])
+        nc.sync.dma_start(codes_view, y_codes[:])
         for q in range(4):
             queue = nc.scalar if q % 2 == 0 else nc.sync
             queue.dma_start(out_2[0, 4 * q : 4 * q + 4, :].bitcast(I32), y_plane[32 * q : 32 * q + 4, :].bitcast(I32))

@@ -17,8 +17,12 @@ GELU = mybir.ActivationFunctionType.Gelu_apprx_tanh
 
 P = 128
 PACK = 4
+QUADRANTS = 4
+LIST_ROWS = 16
 CHUNK = 128
 CHUNKS = S // CHUNK
+LAST = CHUNKS - 1
+ON_GPSIMD = 3
 
 
 def tile_picked_lora_gelu_po_kernel(
@@ -32,7 +36,16 @@ def tile_picked_lora_gelu_po_kernel(
         def sbuf(name, shape, dtype, tag=None):
             return keep.tile(shape, dtype, name=name, tag=tag or name, align_bytes=64)
 
-        offsets = keep.tile([P, S // 16], U16, name="offsets")
+        def live_rows(q):
+            return slice(32 * q, 32 * q + 4)
+
+        def scale_rows(q):
+            return slice(4 * q, 4 * q + 4)
+
+        def chunk_tokens(c):
+            return slice(c * CHUNK, (c + 1) * CHUNK)
+
+        offsets = keep.tile([P, S // LIST_ROWS], U16, name="offsets")
         x_table = sbuf("x_table", [P, T], I32)
         x_scale_table = sbuf("x_scale_table", [P, T], U8)
         w2_cols = [sbuf("w2_cols%d" % u, [P, PACK, H // 2], F32) for u in range(2)]
@@ -42,39 +55,31 @@ def tile_picked_lora_gelu_po_kernel(
         nc.vector.memset(x_scale_table[:].bitcast(I32), 0)
         nc.gpsimd.memset(w_scales[:].bitcast(I32), 0)
 
-        seed = sbuf("seed", [P, 2], F32)
-        nc.gpsimd.memset(seed[:, 0:1], 0.0)
-        nc.scalar.activation(seed[:, 1:2], seed[:, 0:1], GELU)
-
         def load_weight_scales(queue, w, q):
-            rows = w_scales[32 * q : 32 * q + 4, :].bitcast(I32).rearrange("p (u w c) -> p u w c", u=2, w=2)
+            rows = w_scales[live_rows(q), :].bitcast(I32).rearrange("p (u w c) -> p u w c", u=2, w=2)
             scales = (w1_scales, w3_scales)[w]
-            queue.dma_start(rows[:, :, w, :], scales[0, 4 * q : 4 * q + 4, :].bitcast(I32).rearrange("p (u c) -> p u c", u=2))
+            queue.dma_start(rows[:, :, w, :], scales[0, scale_rows(q), :].bitcast(I32).rearrange("p (u c) -> p u c", u=2))
 
         w2_view = w2.rearrange("(p j) c -> p j c", j=PACK)
-        weight_rows = [(w, q) for w in range(2) for q in range(4)]
-        for w, q in weight_rows[:3]:
+        weight_quadrants = [(w, q) for w in range(2) for q in range(QUADRANTS)]
+        for w, q in weight_quadrants[:ON_GPSIMD]:
             load_weight_scales(nc.gpsimd, w, q)
         nc.sync.dma_start(w2_cols[0][:], w2_view[:, :, : H // 2])
         nc.sync.dma_start(offsets[:], offs)
-        for q in range(4):
-            nc.sync.dma_start(
-                x_scale_table[32 * q : 32 * q + 4, :].bitcast(I32), x_scales[0, 4 * q : 4 * q + 4, :].bitcast(I32)
-            )
+        for q in range(QUADRANTS):
+            nc.sync.dma_start(x_scale_table[live_rows(q), :].bitcast(I32), x_scales[0, scale_rows(q), :].bitcast(I32))
         nc.sync.dma_start(w2_cols[1][:], w2_view[:, :, H // 2 :])
         nc.sync.dma_start(x_table[:], x_words[0].rearrange("p n r -> p (n r)").bitcast(I32))
         nc.sync.dma_start(w_raw[:, 0, :].bitcast(I32), w1_words[0].bitcast(I32))
         nc.sync.dma_start(w_raw[:, 1, :].bitcast(I32), w3_words[0].bitcast(I32))
-        for w, q in weight_rows[3:]:
+        for w, q in weight_quadrants[ON_GPSIMD:]:
             load_weight_scales(nc.sync, w, q)
 
         def gather_words(first, count):
             codes = sbuf("x_codes%d" % first, [P, count * CHUNK], U32)
-            nc.vector.tensor_copy(
-                codes[:],
-                x_table[:].bitcast(U32).indirect(offsets[:, first * CHUNK // 16 : (first + count) * CHUNK // 16]),
-            )
-            return [codes[:, c * CHUNK : (c + 1) * CHUNK] for c in range(count)]
+            entries = slice(first * CHUNK // LIST_ROWS, (first + count) * CHUNK // LIST_ROWS)
+            nc.vector.tensor_copy(codes[:], x_table[:].bitcast(U32).indirect(offsets[:, entries]))
+            return [codes[:, chunk_tokens(c)] for c in range(count)]
 
         x_plane = sbuf("x_plane", [P, S], U8)
         nc.vector.tensor_copy(x_plane[:], x_scale_table[:].indirect(offsets[:]))
@@ -90,46 +95,16 @@ def tile_picked_lora_gelu_po_kernel(
             if u == 1:
                 x_codes = gather_words(0, 1)
             for t in range(PACK):
-                first = t * P + u * P // 2
+                cols = slice(t * P + u * P // 2, t * P + (u + 1) * P // 2)
                 nc.vector.quantize_mx(
-                    out=w2_codes[:, first : first + P // 2].bitcast(FP8X4),
-                    scales=w2_plane[:, first : first + P // 2],
+                    out=w2_codes[:, cols].bitcast(FP8X4),
+                    scales=w2_plane[:, cols],
                     in_=w2_bf[:, t * H // 2 : (t + 1) * H // 2],
                 )
 
         x_codes = x_codes + gather_words(1, 1) + gather_words(2, 2)
 
-        def product(out, w, t, codes, plane, c, start, stop):
-            tokens = slice(c * CHUNK, (c + 1) * CHUNK)
-            nc.tensor.matmul_mx(
-                out=out,
-                lhsT=w_dealt[:, w, t, :].bitcast(FP4X4),
-                lhsT_scale=w_plane[:, w, t, :],
-                rhs=codes.bitcast(FP8X4),
-                rhs_scale=plane[:, tokens],
-                start=start,
-                stop=stop,
-            )
-
-        def open_sums(c):
-            tags = ["acc%d" % c] if c < CHUNKS - 1 else ["acc%d" % c, "pre0"]
-            per_bank = PACK // len(tags)
-            banks = [psum.tile([P, per_bank, CHUNK], F32, name="acc%d_%d" % (c, u), tag=tag) for u, tag in enumerate(tags)]
-            for t in range(PACK):
-                product(banks[t // per_bank][:, t % per_bank, :], 0, t, x_codes[c], x_plane, c, t % per_bank == 0, False)
-            return banks
-
-        def close_sums(c):
-            banks = sums[c]
-            per_bank = PACK // len(banks)
-            for t in range(PACK):
-                product(
-                    banks[t // per_bank][:, t % per_bank, :], 1, t, h_codes[:, c * CHUNK : (c + 1) * CHUNK], h_plane, c, False,
-                    t % per_bank == per_bank - 1,
-                )
-
         def hidden(c):
-            tokens = slice(c * CHUNK, (c + 1) * CHUNK)
             pre = psum.tile([P, PACK, CHUNK], F32, name="pre%d" % c, tag="pre%d" % c)
             for t in range(PACK):
                 cols = slice(t * P, (t + 1) * P)
@@ -138,17 +113,18 @@ def tile_picked_lora_gelu_po_kernel(
                     lhsT=w2_codes[:, cols].bitcast(FP8X4),
                     lhsT_scale=w2_plane[:, cols],
                     rhs=x_codes[c].bitcast(FP8X4),
-                    rhs_scale=x_plane[:, tokens],
+                    rhs_scale=x_plane[:, chunk_tokens(c)],
                     start=True,
                     stop=True,
                 )
-            h_bf = sbuf("h_bf%d" % c, [P, CHUNK * PACK], BF16)
+            activated = sbuf("h_bf%d" % c, [P, CHUNK * PACK], BF16)
             nc.scalar.activation(
-                h_bf[:].rearrange("p (n t) -> p n t", t=PACK), pre[:].rearrange("p t n -> p n t"), GELU
+                activated[:].rearrange("p (n t) -> p n t", t=PACK), pre[:].rearrange("p t n -> p n t"), GELU
             )
-            return h_bf
+            return activated
 
         h_bf = [hidden(c) for c in range(CHUNKS)]
+
         w_dealt = sbuf("w_dealt", [P, 2, PACK, 2 * P], U8)
         nc.vector.tensor_copy(
             w_dealt[:].bitcast(U16).rearrange("p w t (g m) -> p w g t m", m=8),
@@ -161,56 +137,62 @@ def tile_picked_lora_gelu_po_kernel(
                 w_scales[:, u * H : (u + 1) * H].rearrange("p (w g m t) -> p w g t m", w=2, m=16, t=PACK),
             )
 
-        h_codes = sbuf("h_codes", [P, S], U32)
+        def weight_passes(banks, w, codes, plane):
+            per_bank = PACK // len(banks)
+            for t in range(PACK):
+                place = t % per_bank
+                nc.tensor.matmul_mx(
+                    out=banks[t // per_bank][:, place, :],
+                    lhsT=w_dealt[:, w, t, :].bitcast(FP4X4),
+                    lhsT_scale=w_plane[:, w, t, :],
+                    rhs=codes.bitcast(FP8X4),
+                    rhs_scale=plane,
+                    start=w == 0 and place == 0,
+                    stop=w == 1 and place == per_bank - 1,
+                )
+
+        h_codes = [sbuf("h_codes%d" % c, [P, CHUNK], U32) for c in range(CHUNKS)]
         h_plane = w_scales[:, :S]
         sums = []
         for c in range(CHUNKS):
-            tokens = slice(c * CHUNK, (c + 1) * CHUNK)
-            nc.vector.quantize_mx(out=h_codes[:, tokens].bitcast(FP8X4), scales=h_plane[:, tokens], in_=h_bf[c][:])
-            sums.append(open_sums(c))
-            close_sums(c)
+            tokens = chunk_tokens(c)
+            nc.vector.quantize_mx(out=h_codes[c][:].bitcast(FP8X4), scales=h_plane[:, tokens], in_=h_bf[c][:])
+            tags = ["acc%d" % c, "pre0"] if c == LAST else ["acc%d" % c]
+            banks = [
+                psum.tile([P, PACK // len(tags), CHUNK], F32, name="acc%d_%d" % (c, u), tag=tag)
+                for u, tag in enumerate(tags)
+            ]
+            weight_passes(banks, 0, x_codes[c], x_plane[:, tokens])
+            weight_passes(banks, 1, h_codes[c][:], h_plane[:, tokens])
+            sums.append(banks)
 
         y_codes = sbuf("y_codes", [P, S], I32)
-        y_plane = sbuf("y_plane", [P, S], U8)
-        out_view = out_0.rearrange("(p t) j -> p t j", t=PACK)
+        y_plane = sbuf("y_plane", [P, S], U8, "h_codes%d" % LAST)
+        out_view = out_0.rearrange("(p t) n -> p t n", t=PACK)
         codes_view = out_1[0].rearrange("p n r -> p (n r)").bitcast(I32)
-
-        y_bf = [sbuf("y_bf%d" % u, [P, count * CHUNK * PACK], BF16) for u, count in enumerate((2, 1, 1))]
-        rounded_chunks = [y_bf[0][:, : CHUNK * PACK], y_bf[0][:, CHUNK * PACK :], y_bf[1][:], y_bf[2][:]]
-
-        def quantize_result(first, count, values):
-            tokens = slice(first * CHUNK, (first + count) * CHUNK)
-            nc.vector.quantize_mx(
-                out=y_codes[:, tokens].bitcast(FP8X4),
-                scales=y_plane[:, tokens],
-                in_=values[:],
-            )
+        y_bf = [sbuf("y_bf%d" % c, [P, CHUNK * PACK], BF16) for c in range(CHUNKS)]
 
         for c in range(CHUNKS):
-            tokens = slice(c * CHUNK, (c + 1) * CHUNK)
             banks = sums[c]
-            y_tile = sbuf("y%d" % c, [P, PACK, CHUNK], F32)
-            y = y_tile[:]
-            rounded = rounded_chunks[c]
-            dst = rounded.rearrange("p (g i t) -> p g t i", i=4, t=PACK)
-            src = y.rearrange("p t (g i) -> p g t i", i=4)
-            if c == CHUNKS - 1:
+            y = sbuf("y%d" % c, [P, PACK, CHUNK], F32)
+            dst = y_bf[c][:].rearrange("p (g i t) -> p g t i", i=4, t=PACK)
+            src = y[:].rearrange("p t (g i) -> p g t i", i=4)
+            if c == LAST:
                 for u in range(2):
                     nc.scalar.copy(y[:, 2 * u : 2 * u + 2, :], banks[u][:])
                 nc.vector.tensor_copy(dst[:, :, 0:2], src[:, :, 0:2])
                 nc.scalar.copy(
-                    rounded.rearrange("p (n t) -> p n t", t=PACK)[:, :, 2:4], banks[1][:].rearrange("p t n -> p n t")
+                    y_bf[c][:].rearrange("p (n t) -> p n t", t=PACK)[:, :, 2:4], banks[1][:].rearrange("p t n -> p n t")
                 )
             else:
-                nc.scalar.copy(y, banks[0][:])
+                nc.scalar.copy(y[:], banks[0][:])
                 nc.vector.tensor_copy(dst, src)
-            nc.sync.dma_start(out_view[:, :, tokens], y)
-            if c == 1:
-                quantize_result(0, 2, y_bf[0])
-        quantize_result(2, 1, y_bf[1])
-        quantize_result(3, 1, y_bf[2])
+            nc.sync.dma_start(out_view[:, :, chunk_tokens(c)], y[:])
+        for c in range(CHUNKS):
+            tokens = chunk_tokens(c)
+            nc.vector.quantize_mx(out=y_codes[:, tokens].bitcast(FP8X4), scales=y_plane[:, tokens], in_=y_bf[c][:])
 
         nc.sync.dma_start(codes_view, y_codes[:])
-        for q in range(4):
+        for q in range(QUADRANTS):
             queue = nc.scalar if q % 2 == 0 else nc.sync
-            queue.dma_start(out_2[0, 4 * q : 4 * q + 4, :].bitcast(I32), y_plane[32 * q : 32 * q + 4, :].bitcast(I32))
+            queue.dma_start(out_2[0, scale_rows(q), :].bitcast(I32), y_plane[live_rows(q), :].bitcast(I32))

@@ -87,20 +87,22 @@ def tile_picked_lora_gelu_po_kernel(
         w2_codes = sbuf("w2_codes", [P, H], U32)
         w2_plane = sbuf("w2_plane", [P, H], U8, "x_scale_table")
         for u in range(2):
-            w2_bf = sbuf("w2_bf%d" % u, [P, PACK * H // 2], BF16)
-            nc.scalar.copy(
-                w2_bf[:].rearrange("p (t m j) -> p m j t", t=PACK, j=PACK),
-                w2_cols[u][:].rearrange("p j (m t) -> p m j t", t=PACK),
-            )
-            if u == 1:
-                x_codes = gather_words(0, 1)
-            for t in range(PACK):
-                cols = slice(t * P + u * P // 2, t * P + (u + 1) * P // 2)
-                nc.vector.quantize_mx(
-                    out=w2_codes[:, cols].bitcast(FP8X4),
-                    scales=w2_plane[:, cols],
-                    in_=w2_bf[:, t * H // 2 : (t + 1) * H // 2],
+            slices = PACK // (u + 1)
+            for first in range(0, PACK, slices):
+                w2_bf = sbuf("w2_bf%d_%d" % (u, first), [P, slices * H // 2], BF16)
+                nc.scalar.copy(
+                    w2_bf[:].rearrange("p (t m j) -> p m j t", t=slices, j=PACK),
+                    w2_cols[u][:].rearrange("p j (m t) -> p m j t", t=PACK)[:, :, :, first : first + slices],
                 )
+                if first > 0:
+                    x_codes = gather_words(0, 1)
+                for t in range(first, first + slices):
+                    cols = slice(t * P + u * P // 2, t * P + (u + 1) * P // 2)
+                    nc.vector.quantize_mx(
+                        out=w2_codes[:, cols].bitcast(FP8X4),
+                        scales=w2_plane[:, cols],
+                        in_=w2_bf[:, (t - first) * H // 2 : (t - first + 1) * H // 2],
+                    )
 
         x_codes = x_codes + gather_words(1, 1) + gather_words(2, 2)
 

@@ -52,7 +52,7 @@ def tile_picked_lora_gelu_po_kernel(
         w_raw = sbuf("w_raw", [P, 2, 2 * H], U8)
         w_scales = sbuf("w_scales", [P, 2 * H], U8)
 
-        nc.vector.memset(x_scale_table[:].bitcast(I32), 0)
+        nc.gpsimd.memset(x_scale_table[:].bitcast(I32), 0)
         nc.gpsimd.memset(w_scales[:].bitcast(I32), 0)
 
         def load_weight_scales(queue, w, q):
@@ -196,5 +196,4 @@ def tile_picked_lora_gelu_po_kernel(
 
         nc.sync.dma_start(codes_view, y_codes[:])
         for q in range(QUADRANTS):
-            queue = nc.scalar if q % 2 == 0 else nc.sync
-            queue.dma_start(out_2[0, scale_rows(q), :].bitcast(I32), y_plane[live_rows(q), :].bitcast(I32))
+            nc.scalar.dma_start(out_2[0, scale_rows(q), :].bitcast(I32), y_plane[live_rows(q), :].bitcast(I32))

@@ -23,6 +23,7 @@ CHUNK = 128
 CHUNKS = S // CHUNK
 LAST = CHUNKS - 1
 ON_GPSIMD = 3
+WARM_PASSES = 2
 
 
 def tile_picked_lora_gelu_po_kernel(
@@ -52,8 +53,13 @@ def tile_picked_lora_gelu_po_kernel(
         w_raw = sbuf("w_raw", [P, 2, 2 * H], U8)
         w_scales = sbuf("w_scales", [P, 2 * H], U8)
 
-        nc.gpsimd.memset(x_scale_table[:].bitcast(I32), 0)
+        nc.vector.memset(x_scale_table[:].bitcast(I32), 0)
         nc.gpsimd.memset(w_scales[:].bitcast(I32), 0)
+
+        table_in = sbuf("table_in", [P, 1], F32)
+        table_out = sbuf("table_out", [P, 1], F32)
+        nc.vector.memset(table_in[:], 0.0)
+        nc.scalar.activation(table_out[:], table_in[:], GELU)
 
         def load_weight_scales(queue, w, q):
             rows = w_scales[live_rows(q), :].bitcast(I32).rearrange("p (u w c) -> p u w c", u=2, w=2)
@@ -95,6 +101,17 @@ def tile_picked_lora_gelu_po_kernel(
                     w2_cols[u][:].rearrange("p j (m t) -> p m j t", t=PACK)[:, :, :, first : first + slices],
                 )
                 if first > 0:
+                    warm = psum.tile([P, 2 * P], F32, name="warm", tag="acc1")
+                    for n in range(WARM_PASSES):
+                        nc.tensor.matmul_mx(
+                            out=warm[:],
+                            lhsT=w2_codes[:, :P].bitcast(FP8X4),
+                            lhsT_scale=w2_plane[:, :P],
+                            rhs=w2_codes[:, : 2 * P].bitcast(FP8X4),
+                            rhs_scale=w2_plane[:, : 2 * P],
+                            start=True,
+                            stop=True,
+                        )
                     x_codes = gather_words(0, 1)
                 for t in range(first, first + slices):
                     cols = slice(t * P + u * P // 2, t * P + (u + 1) * P // 2)
@@ -153,30 +170,33 @@ def tile_picked_lora_gelu_po_kernel(
                     stop=w == 1 and place == per_bank - 1,
                 )
 
-        h_codes = [sbuf("h_codes%d" % c, [P, CHUNK], U32) for c in range(CHUNKS)]
+        ys = [sbuf("y%d" % c, [P, PACK, CHUNK], F32) for c in range(CHUNKS)]
         h_plane = w_scales[:, :S]
         sums = []
         for c in range(CHUNKS):
             tokens = chunk_tokens(c)
-            nc.vector.quantize_mx(out=h_codes[c][:].bitcast(FP8X4), scales=h_plane[:, tokens], in_=h_bf[c][:])
+            if c == LAST:
+                nc.vector.tensor_copy(ys[0][:], sums[0][0][:])
+            h_codes = sbuf("h_codes%d" % c, [P, CHUNK], U32, "h_codes%d" % (c % LAST))
+            nc.vector.quantize_mx(out=h_codes[:].bitcast(FP8X4), scales=h_plane[:, tokens], in_=h_bf[c][:])
             tags = ["acc%d" % c, "pre0"] if c == LAST else ["acc%d" % c]
             banks = [
                 psum.tile([P, PACK // len(tags), CHUNK], F32, name="acc%d_%d" % (c, u), tag=tag)
                 for u, tag in enumerate(tags)
             ]
             weight_passes(banks, 0, x_codes[c], x_plane[:, tokens])
-            weight_passes(banks, 1, h_codes[c][:], h_plane[:, tokens])
+            weight_passes(banks, 1, h_codes[:], h_plane[:, tokens])
             sums.append(banks)
 
         y_codes = sbuf("y_codes", [P, S], I32)
-        y_plane = sbuf("y_plane", [P, S], U8, "h_codes%d" % LAST)
+        y_plane = sbuf("y_plane", [P, S], U8, "h_codes0")
         out_view = out_0.rearrange("(p t) n -> p t n", t=PACK)
         codes_view = out_1[0].rearrange("p n r -> p (n r)").bitcast(I32)
         y_bf = [sbuf("y_bf%d" % c, [P, CHUNK * PACK], BF16) for c in range(CHUNKS)]
 
         for c in range(CHUNKS):
             banks = sums[c]
-            y = sbuf("y%d" % c, [P, PACK, CHUNK], F32)
+            y = ys[c]
             dst = y_bf[c][:].rearrange("p (g i t) -> p g t i", i=4, t=PACK)
             src = y[:].rearrange("p t (g i) -> p g t i", i=4)
             if c == LAST:
@@ -187,7 +207,8 @@ def tile_picked_lora_gelu_po_kernel(
                     y_bf[c][:].rearrange("p (n t) -> p n t", t=PACK)[:, :, 2:4], banks[1][:].rearrange("p t n -> p n t")
                 )
             else:
-                nc.scalar.copy(y[:], banks[0][:])
+                if c > 0:
+                    nc.scalar.copy(y[:], banks[0][:])
                 nc.vector.tensor_copy(dst, src)
             nc.sync.dma_start(out_view[:, :, chunk_tokens(c)], y[:])
         for c in range(CHUNKS):
@@ -196,4 +217,5 @@ def tile_picked_lora_gelu_po_kernel(
 
         nc.sync.dma_start(codes_view, y_codes[:])
         for q in range(QUADRANTS):
-            nc.scalar.dma_start(out_2[0, scale_rows(q), :].bitcast(I32), y_plane[live_rows(q), :].bitcast(I32))
+            queue = nc.scalar if q % 2 == 0 else nc.sync
+            queue.dma_start(out_2[0, scale_rows(q), :].bitcast(I32), y_plane[live_rows(q), :].bitcast(I32))

@@ -23,7 +23,6 @@ CHUNK = 128
 CHUNKS = S // CHUNK
 LAST = CHUNKS - 1
 ON_GPSIMD = 3
-WARM_PASSES = 2
 
 
 def tile_picked_lora_gelu_po_kernel(
@@ -55,11 +54,6 @@ def tile_picked_lora_gelu_po_kernel(
 
         nc.vector.memset(x_scale_table[:].bitcast(I32), 0)
         nc.gpsimd.memset(w_scales[:].bitcast(I32), 0)
-
-        table_in = sbuf("table_in", [P, 1], F32)
-        table_out = sbuf("table_out", [P, 1], F32)
-        nc.vector.memset(table_in[:], 0.0)
-        nc.scalar.activation(table_out[:], table_in[:], GELU)
 
         def load_weight_scales(queue, w, q):
             rows = w_scales[live_rows(q), :].bitcast(I32).rearrange("p (u w c) -> p u w c", u=2, w=2)
@@ -101,17 +95,6 @@ def tile_picked_lora_gelu_po_kernel(
                     w2_cols[u][:].rearrange("p j (m t) -> p m j t", t=PACK)[:, :, :, first : first + slices],
                 )
                 if first > 0:
-                    warm = psum.tile([P, 2 * P], F32, name="warm", tag="acc1")
-                    for n in range(WARM_PASSES):
-                        nc.tensor.matmul_mx(
-                            out=warm[:],
-                            lhsT=w2_codes[:, :P].bitcast(FP8X4),
-                            lhsT_scale=w2_plane[:, :P],
-                            rhs=w2_codes[:, : 2 * P].bitcast(FP8X4),
-                            rhs_scale=w2_plane[:, : 2 * P],
-                            start=True,
-                            stop=True,
-                        )
                     x_codes = gather_words(0, 1)
                 for t in range(first, first + slices):
                     cols = slice(t * P + u * P // 2, t * P + (u + 1) * P // 2)

@@ -75,10 +75,16 @@ def tile_picked_lora_gelu_po_kernel(
         for w, q in weight_quadrants[ON_GPSIMD:]:
             load_weight_scales(nc.sync, w, q)
 
+        warm = sbuf("warm", [P, 1], F32)
+        nc.scalar.activation(warm[:], w2_cols[0][:, 0, 0:1], GELU)
+
+        x_pair = sbuf("x_pair", [P, 2 * CHUNK], U32)
+        x_rest = sbuf("x_rest", [P, 2 * CHUNK], U32)
+
         def gather_words(first, count):
-            codes = sbuf("x_codes%d" % first, [P, count * CHUNK], U32)
+            codes = (x_pair, x_rest)[first // 2][:, first % 2 * CHUNK : (first % 2 + count) * CHUNK]
             entries = slice(first * CHUNK // LIST_ROWS, (first + count) * CHUNK // LIST_ROWS)
-            nc.vector.tensor_copy(codes[:], x_table[:].bitcast(U32).indirect(offsets[:, entries]))
+            nc.vector.tensor_copy(codes, x_table[:].bitcast(U32).indirect(offsets[:, entries]))
             return [codes[:, chunk_tokens(c)] for c in range(count)]
 
         x_plane = sbuf("x_plane", [P, S], U8)
@@ -139,12 +145,11 @@ def tile_picked_lora_gelu_po_kernel(
                 w_scales[:, u * H : (u + 1) * H].rearrange("p (w g m t) -> p w g t m", w=2, m=16, t=PACK),
             )
 
-        def weight_passes(banks, w, codes, plane):
-            per_bank = PACK // len(banks)
-            for t in range(PACK):
-                place = t % per_bank
+        def weight_passes(bank, w, codes, plane, slices):
+            per_bank = len(slices)
+            for place, t in enumerate(slices):
                 nc.tensor.matmul_mx(
-                    out=banks[t // per_bank][:, place, :],
+                    out=bank[:, place, :],
                     lhsT=w_dealt[:, w, t, :].bitcast(FP4X4),
                     lhsT_scale=w_plane[:, w, t, :],
                     rhs=codes.bitcast(FP8X4),
@@ -153,50 +158,74 @@ def tile_picked_lora_gelu_po_kernel(
                     stop=w == 1 and place == per_bank - 1,
                 )
 
-        ys = [sbuf("y%d" % c, [P, PACK, CHUNK], F32) for c in range(CHUNKS)]
         h_plane = w_scales[:, :S]
+        pair = slice(0, 2 * CHUNK)
+        h_pair = sbuf("h_pair", [P, 2 * CHUNK], U32)
+        for c in range(2):
+            nc.vector.quantize_mx(
+                out=h_pair[:, chunk_tokens(c)].bitcast(FP8X4), scales=h_plane[:, chunk_tokens(c)], in_=h_bf[c][:]
+            )
+        pair_banks = []
+        for tag, slices in (("acc0", range(0, 2)), ("acc1", range(2, 3)), ("pre1", range(3, 4))):
+            bank = psum.tile([P, len(slices), 2 * CHUNK], F32, name="pair%d" % slices[0], tag=tag)
+            weight_passes(bank, 0, x_pair[:], x_plane[:, pair], slices)
+            weight_passes(bank, 1, h_pair[:], h_plane[:, pair], slices)
+            pair_banks.append(bank)
         sums = []
-        for c in range(CHUNKS):
+        for c in range(2, CHUNKS):
             tokens = chunk_tokens(c)
-            if c == LAST:
-                nc.vector.tensor_copy(ys[0][:], sums[0][0][:])
-            h_codes = sbuf("h_codes%d" % c, [P, CHUNK], U32, "h_codes%d" % (c % LAST))
+            h_codes = sbuf("h_codes%d" % c, [P, CHUNK], U32)
             nc.vector.quantize_mx(out=h_codes[:].bitcast(FP8X4), scales=h_plane[:, tokens], in_=h_bf[c][:])
             tags = ["acc%d" % c, "pre0"] if c == LAST else ["acc%d" % c]
             banks = [
                 psum.tile([P, PACK // len(tags), CHUNK], F32, name="acc%d_%d" % (c, u), tag=tag)
                 for u, tag in enumerate(tags)
             ]
-            weight_passes(banks, 0, x_codes[c], x_plane[:, tokens])
-            weight_passes(banks, 1, h_codes[:], h_plane[:, tokens])
+            per_bank = PACK // len(banks)
+            for w, codes, plane in ((0, x_codes[c], x_plane[:, tokens]), (1, h_codes[:], h_plane[:, tokens])):
+                for u, bank in enumerate(banks):
+                    weight_passes(bank, w, codes, plane, range(u * per_bank, (u + 1) * per_bank))
             sums.append(banks)
 
         y_codes = sbuf("y_codes", [P, S], I32)
-        y_plane = sbuf("y_plane", [P, S], U8, "h_codes0")
+        y_plane = sbuf("y_plane", [P, S], U8, "h_codes3")
         out_view = out_0.rearrange("(p t) n -> p t n", t=PACK)
         codes_view = out_1[0].rearrange("p n r -> p (n r)").bitcast(I32)
-        y_bf = [sbuf("y_bf%d" % c, [P, CHUNK * PACK], BF16) for c in range(CHUNKS)]
 
-        for c in range(CHUNKS):
-            banks = sums[c]
-            y = ys[c]
-            dst = y_bf[c][:].rearrange("p (g i t) -> p g t i", i=4, t=PACK)
+        y_pair = sbuf("y_pair", [P, PACK, 2 * CHUNK], F32)
+        nc.scalar.copy(y_pair[:, 0:2, :], pair_banks[0][:])
+        nc.sync.dma_start(out_view[:, 0:2, pair], y_pair[:, 0:2, :])
+        nc.vector.tensor_copy(y_pair[:, 2:3, :], pair_banks[1][:])
+        nc.scalar.copy(y_pair[:, 3:4, :], pair_banks[2][:])
+        nc.sync.dma_start(out_view[:, 2:4, pair], y_pair[:, 2:4, :])
+        rounded = []
+        for c in range(2):
+            y_bf = sbuf("y_bf%d" % c, [P, CHUNK * PACK], BF16)
+            nc.vector.tensor_copy(
+                y_bf[:].rearrange("p (g i t) -> p g t i", i=4, t=PACK),
+                y_pair[:, :, chunk_tokens(c)].rearrange("p t (g i) -> p g t i", i=4),
+            )
+            rounded.append((chunk_tokens(c), y_bf))
+        for c in range(2, CHUNKS):
+            banks = sums[c - 2]
+            y = sbuf("y%d" % c, [P, PACK, CHUNK], F32)
+            y_bf = sbuf("y_bf%d" % c, [P, CHUNK * PACK], BF16)
+            dst = y_bf[:].rearrange("p (g i t) -> p g t i", i=4, t=PACK)
             src = y[:].rearrange("p t (g i) -> p g t i", i=4)
             if c == LAST:
                 for u in range(2):
                     nc.scalar.copy(y[:, 2 * u : 2 * u + 2, :], banks[u][:])
                 nc.vector.tensor_copy(dst[:, :, 0:2], src[:, :, 0:2])
                 nc.scalar.copy(
-                    y_bf[c][:].rearrange("p (n t) -> p n t", t=PACK)[:, :, 2:4], banks[1][:].rearrange("p t n -> p n t")
+                    y_bf[:].rearrange("p (n t) -> p n t", t=PACK)[:, :, 2:4], banks[1][:].rearrange("p t n -> p n t")
                 )
             else:
-                if c > 0:
-                    nc.scalar.copy(y[:], banks[0][:])
+                nc.scalar.copy(y[:], banks[0][:])
                 nc.vector.tensor_copy(dst, src)
             nc.sync.dma_start(out_view[:, :, chunk_tokens(c)], y[:])
-        for c in range(CHUNKS):
-            tokens = chunk_tokens(c)
-            nc.vector.quantize_mx(out=y_codes[:, tokens].bitcast(FP8X4), scales=y_plane[:, tokens], in_=y_bf[c][:])
+            rounded.append((chunk_tokens(c), y_bf))
+        for tokens, y_bf in rounded:
+            nc.vector.quantize_mx(out=y_codes[:, tokens].bitcast(FP8X4), scales=y_plane[:, tokens], in_=y_bf[:])
 
         nc.sync.dma_start(codes_view, y_codes[:])
         for q in range(QUADRANTS):

@@ -159,73 +159,81 @@ def tile_picked_lora_gelu_po_kernel(
                 )
 
         h_plane = w_scales[:, :S]
-        pair = slice(0, 2 * CHUNK)
-        h_pair = sbuf("h_pair", [P, 2 * CHUNK], U32)
-        for c in range(2):
-            nc.vector.quantize_mx(
-                out=h_pair[:, chunk_tokens(c)].bitcast(FP8X4), scales=h_plane[:, chunk_tokens(c)], in_=h_bf[c][:]
-            )
-        pair_banks = []
-        for tag, slices in (("acc0", range(0, 2)), ("acc1", range(2, 3)), ("pre1", range(3, 4))):
-            bank = psum.tile([P, len(slices), 2 * CHUNK], F32, name="pair%d" % slices[0], tag=tag)
-            weight_passes(bank, 0, x_pair[:], x_plane[:, pair], slices)
-            weight_passes(bank, 1, h_pair[:], h_plane[:, pair], slices)
-            pair_banks.append(bank)
-        sums = []
-        for c in range(2, CHUNKS):
-            tokens = chunk_tokens(c)
-            h_codes = sbuf("h_codes%d" % c, [P, CHUNK], U32)
-            nc.vector.quantize_mx(out=h_codes[:].bitcast(FP8X4), scales=h_plane[:, tokens], in_=h_bf[c][:])
-            tags = ["acc%d" % c, "pre0"] if c == LAST else ["acc%d" % c]
-            banks = [
-                psum.tile([P, PACK // len(tags), CHUNK], F32, name="acc%d_%d" % (c, u), tag=tag)
-                for u, tag in enumerate(tags)
-            ]
-            per_bank = PACK // len(banks)
-            for w, codes, plane in ((0, x_codes[c], x_plane[:, tokens]), (1, h_codes[:], h_plane[:, tokens])):
-                for u, bank in enumerate(banks):
-                    weight_passes(bank, w, codes, plane, range(u * per_bank, (u + 1) * per_bank))
-            sums.append(banks)
-
+        h_pairs = [sbuf("h_pair%d" % u, [P, 2 * CHUNK], U32) for u in range(2)]
+        x_pairs = [x_pair, x_rest]
+        y_pairs = [sbuf("y_pair%d" % u, [P, PACK, 2 * CHUNK], F32) for u in range(2)]
+        y_bf = [sbuf("y_bf%d" % c, [P, CHUNK * PACK], BF16) for c in range(CHUNKS)]
         y_codes = sbuf("y_codes", [P, S], I32)
-        y_plane = sbuf("y_plane", [P, S], U8, "h_codes3")
+        y_plane = sbuf("y_plane", [P, S], U8)
         out_view = out_0.rearrange("(p t) n -> p t n", t=PACK)
         codes_view = out_1[0].rearrange("p n r -> p (n r)").bitcast(I32)
 
-        y_pair = sbuf("y_pair", [P, PACK, 2 * CHUNK], F32)
-        nc.scalar.copy(y_pair[:, 0:2, :], pair_banks[0][:])
-        nc.sync.dma_start(out_view[:, 0:2, pair], y_pair[:, 0:2, :])
-        nc.vector.tensor_copy(y_pair[:, 2:3, :], pair_banks[1][:])
-        nc.scalar.copy(y_pair[:, 3:4, :], pair_banks[2][:])
-        nc.sync.dma_start(out_view[:, 2:4, pair], y_pair[:, 2:4, :])
-        rounded = []
-        for c in range(2):
-            y_bf = sbuf("y_bf%d" % c, [P, CHUNK * PACK], BF16)
-            nc.vector.tensor_copy(
-                y_bf[:].rearrange("p (g i t) -> p g t i", i=4, t=PACK),
-                y_pair[:, :, chunk_tokens(c)].rearrange("p t (g i) -> p g t i", i=4),
+        def quantise_h(c):
+            nc.vector.quantize_mx(
+                out=h_pairs[c // 2][:, chunk_tokens(c % 2)].bitcast(FP8X4),
+                scales=h_plane[:, chunk_tokens(c)],
+                in_=h_bf[c][:],
             )
-            rounded.append((chunk_tokens(c), y_bf))
+
+        def add_up(tag, pair, rows, local):
+            tokens = slice(2 * CHUNK * pair + local.start, 2 * CHUNK * pair + local.stop)
+            bank = psum.tile(
+                [P, rows.stop - rows.start, local.stop - local.start],
+                F32,
+                name="acc%d_%d_%d" % (pair, rows.start, local.start),
+                tag=tag,
+            )
+            slices = range(rows.start, rows.stop)
+            weight_passes(bank, 0, x_pairs[pair][:, local], x_plane[:, tokens], slices)
+            weight_passes(bank, 1, h_pairs[pair][:, local], h_plane[:, tokens], slices)
+            return bank
+
+        def store_y(pair, rows):
+            nc.sync.dma_start(out_view[:, rows, 2 * CHUNK * pair : 2 * CHUNK * (pair + 1)], y_pairs[pair][:, rows, :])
+
+        def round_y(c, rows):
+            nc.vector.tensor_copy(
+                y_bf[c][:].rearrange("p (g i t) -> p g t i", i=4, t=PACK)[:, :, rows],
+                y_pairs[c // 2][:, rows, chunk_tokens(c % 2)].rearrange("p t (g i) -> p g t i", i=4),
+            )
+
+        def quantise_y(c):
+            tokens = chunk_tokens(c)
+            nc.vector.quantize_mx(out=y_codes[:, tokens].bitcast(FP8X4), scales=y_plane[:, tokens], in_=y_bf[c][:])
+
+        both, low, high = slice(0, 2 * CHUNK), slice(0, 2), slice(2, 4)
+        for c in range(CHUNKS):
+            quantise_h(c)
+        first = [add_up("acc0", 0, low, both), add_up("acc1", 0, slice(2, 3), both), add_up("pre1", 0, slice(3, 4), both)]
+        last = [
+            add_up("acc2", 1, slice(0, 1), both),
+            add_up("acc3", 1, slice(1, 2), both),
+            add_up("pre0", 1, high, chunk_tokens(0)),
+            add_up("acc0", 1, high, chunk_tokens(1)),
+        ]
+
+        nc.scalar.copy(y_pairs[0][:, low, :], first[0][:])
+        store_y(0, low)
+        nc.vector.tensor_copy(y_pairs[0][:, 2:3, :], first[1][:])
+        nc.scalar.copy(y_pairs[0][:, 3:4, :], first[2][:])
+        store_y(0, high)
+        for c in range(2):
+            round_y(c, slice(0, PACK))
+        for t in range(2):
+            nc.scalar.copy(y_pairs[1][:, t : t + 1, :], last[t][:])
+        store_y(1, low)
+        nc.scalar.copy(y_pairs[1][:, high, chunk_tokens(0)], last[2][:])
+        nc.scalar.copy(y_pairs[1][:, high, chunk_tokens(1)], last[3][:])
+        store_y(1, high)
+        round_y(3, low)
+        quantise_y(0)
+        round_y(2, slice(0, PACK))
+        quantise_y(1)
+        nc.scalar.copy(
+            y_bf[3][:].rearrange("p (n t) -> p n t", t=PACK)[:, :, high], last[3][:].rearrange("p t n -> p n t")
+        )
         for c in range(2, CHUNKS):
-            banks = sums[c - 2]
-            y = sbuf("y%d" % c, [P, PACK, CHUNK], F32)
-            y_bf = sbuf("y_bf%d" % c, [P, CHUNK * PACK], BF16)
-            dst = y_bf[:].rearrange("p (g i t) -> p g t i", i=4, t=PACK)
-            src = y[:].rearrange("p t (g i) -> p g t i", i=4)
-            if c == LAST:
-                for u in range(2):
-                    nc.scalar.copy(y[:, 2 * u : 2 * u + 2, :], banks[u][:])
-                nc.vector.tensor_copy(dst[:, :, 0:2], src[:, :, 0:2])
-                nc.scalar.copy(
-                    y_bf[:].rearrange("p (n t) -> p n t", t=PACK)[:, :, 2:4], banks[1][:].rearrange("p t n -> p n t")
-                )
-            else:
-                nc.scalar.copy(y[:], banks[0][:])
-                nc.vector.tensor_copy(dst, src)
-            nc.sync.dma_start(out_view[:, :, chunk_tokens(c)], y[:])
-            rounded.append((chunk_tokens(c), y_bf))
-        for tokens, y_bf in rounded:
-            nc.vector.quantize_mx(out=y_codes[:, tokens].bitcast(FP8X4), scales=y_plane[:, tokens], in_=y_bf[:])
+            quantise_y(c)
 
         nc.sync.dma_start(codes_view, y_codes[:])
         for q in range(QUADRANTS):

@@ -49,7 +49,7 @@ def tile_picked_lora_gelu_po_kernel(
         x_table = sbuf("x_table", [P, T], I32)
         x_scale_table = sbuf("x_scale_table", [P, T], U8)
         w2_cols = [sbuf("w2_cols%d" % u, [P, PACK, H // 2], F32) for u in range(2)]
-        w_raw = sbuf("w_raw", [P, 2, 2 * H], U8)
+        w_raw = [sbuf("w_raw%d" % w, [P, 2 * H], U8) for w in range(2)]
         w_scales = sbuf("w_scales", [P, 2 * H], U8)
 
         nc.vector.memset(x_scale_table[:].bitcast(I32), 0)
@@ -70,8 +70,8 @@ def tile_picked_lora_gelu_po_kernel(
             nc.sync.dma_start(x_scale_table[live_rows(q), :].bitcast(I32), x_scales[0, scale_rows(q), :].bitcast(I32))
         nc.sync.dma_start(w2_cols[1][:], w2_view[:, :, H // 2 :])
         nc.sync.dma_start(x_table[:], x_words[0].rearrange("p n r -> p (n r)").bitcast(I32))
-        nc.sync.dma_start(w_raw[:, 0, :].bitcast(I32), w1_words[0].bitcast(I32))
-        nc.sync.dma_start(w_raw[:, 1, :].bitcast(I32), w3_words[0].bitcast(I32))
+        nc.sync.dma_start(w_raw[0][:].bitcast(I32), w1_words[0].bitcast(I32))
+        nc.sync.dma_start(w_raw[1][:].bitcast(I32), w3_words[0].bitcast(I32))
         for w, q in weight_quadrants[ON_GPSIMD:]:
             load_weight_scales(nc.sync, w, q)
 
@@ -112,6 +112,16 @@ def tile_picked_lora_gelu_po_kernel(
 
         x_codes = x_codes + gather_words(1, 1) + gather_words(2, 2)
 
+        w_dealt = [sbuf("w_dealt%d" % w, [P, PACK, 2 * P], U8) for w in range(2)]
+
+        def deal_words(copy, w):
+            copy(
+                w_dealt[w][:].bitcast(U16).rearrange("p t (g m) -> p g t m", m=8),
+                w_raw[w][:].bitcast(U16).rearrange("p (g m t) -> p g t m", m=8, t=PACK),
+            )
+
+        deal_words(nc.scalar.copy, 0)
+
         def hidden(c):
             pre = psum.tile([P, PACK, CHUNK], F32, name="pre%d" % c, tag="pre%d" % c)
             for t in range(PACK):
@@ -133,11 +143,7 @@ def tile_picked_lora_gelu_po_kernel(
 
         h_bf = [hidden(c) for c in range(CHUNKS)]
 
-        w_dealt = sbuf("w_dealt", [P, 2, PACK, 2 * P], U8)
-        nc.vector.tensor_copy(
-            w_dealt[:].bitcast(U16).rearrange("p w t (g m) -> p w g t m", m=8),
-            w_raw[:].bitcast(U16).rearrange("p w (g m t) -> p w g t m", m=8, t=PACK),
-        )
+        deal_words(nc.vector.tensor_copy, 1)
         w_plane = sbuf("w_plane", [P, 2, PACK, P], U8)
         for u in range(2):
             nc.vector.tensor_copy(
@@ -150,7 +156,7 @@ def tile_picked_lora_gelu_po_kernel(
             for place, t in enumerate(slices):
                 nc.tensor.matmul_mx(
                     out=bank[:, place, :],
-                    lhsT=w_dealt[:, w, t, :].bitcast(FP4X4),
+                    lhsT=w_dealt[w][:, t, :].bitcast(FP4X4),
                     lhsT_scale=w_plane[:, w, t, :],
                     rhs=codes.bitcast(FP8X4),
                     rhs_scale=plane,

@@ -36,6 +36,11 @@ def tile_picked_lora_gelu_po_kernel(
         def sbuf(name, shape, dtype, tag=None):
             return keep.tile(shape, dtype, name=name, tag=tag or name, align_bytes=64)
 
+        late = ctx.enter_context(tc.tile_pool(name="late", bufs=1))
+
+        def placed(name, shape, dtype, offset):
+            return late.tile(shape, dtype, name=name, tag=name, align_bytes=64, offset=offset)
+
         def live_rows(q):
             return slice(32 * q, 32 * q + 4)
 
@@ -50,7 +55,7 @@ def tile_picked_lora_gelu_po_kernel(
         x_scale_table = sbuf("x_scale_table", [P, T], U8)
         w2_cols = [sbuf("w2_cols%d" % u, [P, PACK, H // 2], F32) for u in range(2)]
         w_raw = [sbuf("w_raw%d" % w, [P, 2 * H], U8) for w in range(2)]
-        w_scales = sbuf("w_scales", [P, 2 * H], U8)
+        w_scales = placed("w_scales", [P, 4 * H], U8, 1024)[:, : 2 * H]
 
         nc.vector.memset(x_scale_table[:].bitcast(I32), 0)
         nc.gpsimd.memset(w_scales[:].bitcast(I32), 0)
@@ -71,9 +76,9 @@ def tile_picked_lora_gelu_po_kernel(
         nc.sync.dma_start(w2_cols[1][:], w2_view[:, :, H // 2 :])
         nc.sync.dma_start(x_table[:], x_words[0].rearrange("p n r -> p (n r)").bitcast(I32))
         nc.sync.dma_start(w_raw[0][:].bitcast(I32), w1_words[0].bitcast(I32))
-        nc.sync.dma_start(w_raw[1][:].bitcast(I32), w3_words[0].bitcast(I32))
         for w, q in weight_quadrants[ON_GPSIMD:]:
             load_weight_scales(nc.sync, w, q)
+        nc.sync.dma_start(w_raw[1][:].bitcast(I32), w3_words[0].bitcast(I32))
 
         warm = sbuf("warm", [P, 1], F32)
         nc.scalar.activation(warm[:], w2_cols[0][:, 0, 0:1], GELU)
@@ -121,6 +126,15 @@ def tile_picked_lora_gelu_po_kernel(
             )
 
         deal_words(nc.scalar.copy, 0)
+        w_plane = sbuf("w_plane", [P, 2, PACK, P], U8)
+
+        def deal_weights():
+            for u in range(2):
+                nc.vector.tensor_copy(
+                    w_plane[:, :, :, u * P // 2 : (u + 1) * P // 2].rearrange("p w t (g m) -> p w g t m", m=16),
+                    w_scales[:, u * H : (u + 1) * H].rearrange("p (w g m t) -> p w g t m", w=2, m=16, t=PACK),
+                )
+            deal_words(nc.vector.tensor_copy, 1)
 
         def hidden(c):
             pre = psum.tile([P, PACK, CHUNK], F32, name="pre%d" % c, tag="pre%d" % c)
@@ -135,7 +149,12 @@ def tile_picked_lora_gelu_po_kernel(
                     start=True,
                     stop=True,
                 )
-            activated = sbuf("h_bf%d" % c, [P, CHUNK * PACK], BF16)
+            if c == 2:
+                deal_weights()
+            if c >= 2:
+                activated = placed("h_bf%d" % c, [P, CHUNK * PACK], BF16, 1024 * c - 512)
+            else:
+                activated = sbuf("h_bf%d" % c, [P, CHUNK * PACK], BF16)
             nc.scalar.activation(
                 activated[:].rearrange("p (n t) -> p n t", t=PACK), pre[:].rearrange("p t n -> p n t"), GELU
             )
@@ -143,15 +162,7 @@ def tile_picked_lora_gelu_po_kernel(
 
         h_bf = [hidden(c) for c in range(CHUNKS)]
 
-        deal_words(nc.vector.tensor_copy, 1)
-        w_plane = sbuf("w_plane", [P, 2, PACK, P], U8)
-        for u in range(2):
-            nc.vector.tensor_copy(
-                w_plane[:, :, :, u * P // 2 : (u + 1) * P // 2].rearrange("p w t (g m) -> p w g t m", m=16),
-                w_scales[:, u * H : (u + 1) * H].rearrange("p (w g m t) -> p w g t m", w=2, m=16, t=PACK),
-            )
-
-        def weight_passes(bank, w, codes, plane, slices):
+        def weight_passes(bank, w, codes, plane, slices, opener=0):
             per_bank = len(slices)
             for place, t in enumerate(slices):
                 nc.tensor.matmul_mx(
@@ -160,12 +171,13 @@ def tile_picked_lora_gelu_po_kernel(
                     lhsT_scale=w_plane[:, w, t, :],
                     rhs=codes.bitcast(FP8X4),
                     rhs_scale=plane,
-                    start=w == 0 and place == 0,
-                    stop=w == 1 and place == per_bank - 1,
+                    start=w == opener and place == 0,
+                    stop=w != opener and place == per_bank - 1,
                 )
 
-        h_plane = w_scales[:, :S]
-        h_pairs = [sbuf("h_pair%d" % u, [P, 2 * CHUNK], U32) for u in range(2)]
+        h_planes = [sbuf("h_plane%d" % u, [P, 2 * CHUNK], U8)[:] for u in range(2)]
+        x_planes = [x_plane[:, : 2 * CHUNK], x_plane[:, 2 * CHUNK :]]
+        h_pairs = [placed("h_pair0", [P, 2 * CHUNK], U32, 512), sbuf("h_pair1", [P, 2 * CHUNK], U32)]
         x_pairs = [x_pair, x_rest]
         y_pairs = [sbuf("y_pair%d" % u, [P, PACK, 2 * CHUNK], F32) for u in range(2)]
         y_bf = [sbuf("y_bf%d" % c, [P, CHUNK * PACK], BF16) for c in range(CHUNKS)]
@@ -177,12 +189,11 @@ def tile_picked_lora_gelu_po_kernel(
         def quantise_h(c):
             nc.vector.quantize_mx(
                 out=h_pairs[c // 2][:, chunk_tokens(c % 2)].bitcast(FP8X4),
-                scales=h_plane[:, chunk_tokens(c)],
+                scales=h_planes[c // 2][:, chunk_tokens(c % 2)],
                 in_=h_bf[c][:],
             )
 
-        def add_up(tag, pair, rows, local):
-            tokens = slice(2 * CHUNK * pair + local.start, 2 * CHUNK * pair + local.stop)
+        def open_piece(tag, pair, rows, local):
             bank = psum.tile(
                 [P, rows.stop - rows.start, local.stop - local.start],
                 F32,
@@ -190,8 +201,11 @@ def tile_picked_lora_gelu_po_kernel(
                 tag=tag,
             )
             slices = range(rows.start, rows.stop)
-            weight_passes(bank, 0, x_pairs[pair][:, local], x_plane[:, tokens], slices)
-            weight_passes(bank, 1, h_pairs[pair][:, local], h_plane[:, tokens], slices)
+            weight_passes(bank, 0, x_pairs[pair][:, local], x_planes[pair][:, local], slices)
+            return bank, h_pairs[pair][:, local], h_planes[pair][:, local], slices
+
+        def close_piece(bank, codes, plane, slices):
+            weight_passes(bank, 1, codes, plane, slices)
             return bank
 
         def store_y(pair, rows):
@@ -208,38 +222,49 @@ def tile_picked_lora_gelu_po_kernel(
             nc.vector.quantize_mx(out=y_codes[:, tokens].bitcast(FP8X4), scales=y_plane[:, tokens], in_=y_bf[c][:])
 
         both, low, high = slice(0, 2 * CHUNK), slice(0, 2), slice(2, 4)
-        for c in range(CHUNKS):
+        for c in range(LAST):
             quantise_h(c)
-        first = [add_up("acc0", 0, low, both), add_up("acc1", 0, slice(2, 3), both), add_up("pre1", 0, slice(3, 4), both)]
-        last = [
-            add_up("acc2", 1, slice(0, 1), both),
-            add_up("acc3", 1, slice(1, 2), both),
-            add_up("pre0", 1, high, chunk_tokens(0)),
-            add_up("acc0", 1, high, chunk_tokens(1)),
-        ]
+        def late_piece(tag, c):
+            bank = psum.tile([P, 2, CHUNK], F32, name="late%d" % c, tag=tag)
+            local = chunk_tokens(c % 2)
+            weight_passes(bank, 1, h_pairs[1][:, local], h_planes[1][:, local], range(2, PACK), 1)
+            weight_passes(bank, 0, x_pairs[1][:, local], x_planes[1][:, local], range(2, PACK), 1)
+            return bank
 
-        nc.scalar.copy(y_pairs[0][:, low, :], first[0][:])
+        first = [open_piece("acc%d" % t, 0, slice(t, t + 1), both) for t in range(LAST)]
+        first = [close_piece(*piece) for piece in first]
+        first.append(psum.tile([P, 1, 2 * CHUNK], F32, name="first3", tag="acc3"))
+        weight_passes(first[LAST], 1, h_pairs[0][:], h_planes[0], [LAST], 1)
+        weight_passes(first[LAST], 0, x_pairs[0][:], x_planes[0], [LAST], 1)
+        nc.vector.tensor_copy(y_pairs[0][:, 0:1, :], first[0][:])
+        quantise_h(LAST)
+        nc.scalar.copy(y_pairs[0][:, 1:2, :], first[1][:])
         store_y(0, low)
-        nc.vector.tensor_copy(y_pairs[0][:, 2:3, :], first[1][:])
-        nc.scalar.copy(y_pairs[0][:, 3:4, :], first[2][:])
+        nc.scalar.copy(y_pairs[0][:, 2:3, :], first[2][:])
+        nc.scalar.copy(y_pairs[0][:, 3:4, :], first[3][:])
         store_y(0, high)
-        for c in range(2):
-            round_y(c, slice(0, PACK))
+
+        last = [open_piece("pre%d" % (2 + t), 1, slice(t, t + 1), both) for t in range(2)]
+        fourth = open_piece("acc0", 1, high, chunk_tokens(1))
+        last = [close_piece(*piece) for piece in last]
+        last = last + [late_piece("pre0", 2), close_piece(*fourth)]
         for t in range(2):
             nc.scalar.copy(y_pairs[1][:, t : t + 1, :], last[t][:])
         store_y(1, low)
-        nc.scalar.copy(y_pairs[1][:, high, chunk_tokens(0)], last[2][:])
+        nc.vector.tensor_copy(y_pairs[1][:, high, chunk_tokens(0)], last[2][:])
         nc.scalar.copy(y_pairs[1][:, high, chunk_tokens(1)], last[3][:])
         store_y(1, high)
+        for c in range(2):
+            round_y(c, slice(0, PACK))
         round_y(3, low)
-        quantise_y(0)
         round_y(2, slice(0, PACK))
+        quantise_y(0)
         quantise_y(1)
         nc.scalar.copy(
             y_bf[3][:].rearrange("p (n t) -> p n t", t=PACK)[:, :, high], last[3][:].rearrange("p t n -> p n t")
         )
-        for c in range(2, CHUNKS):
-            quantise_y(c)
+        quantise_y(3)
+        quantise_y(2)
 
         nc.sync.dma_start(codes_view, y_codes[:])
         for q in range(QUADRANTS):

@@ -23,6 +23,7 @@ CHUNK = 128
 CHUNKS = S // CHUNK
 LAST = CHUNKS - 1
 ON_GPSIMD = 3
+WARM_UPS = 4
 
 
 def tile_picked_lora_gelu_po_kernel(
@@ -106,6 +107,17 @@ def tile_picked_lora_gelu_po_kernel(
                     w2_cols[u][:].rearrange("p j (m t) -> p m j t", t=PACK)[:, :, :, first : first + slices],
                 )
                 if first > 0:
+                    spare = psum.tile([P, CHUNK], F32, name="spare", tag="pre3")
+                    for i in range(WARM_UPS):
+                        nc.tensor.matmul_mx(
+                            out=spare[:],
+                            lhsT=w2_codes[:, :P].bitcast(FP8X4),
+                            lhsT_scale=w2_plane[:, :P],
+                            rhs=w2_codes[:, :P].bitcast(FP8X4),
+                            rhs_scale=w2_plane[:, :P],
+                            start=True,
+                            stop=True,
+                        )
                     x_codes = gather_words(0, 1)
                 for t in range(first, first + slices):
                     cols = slice(t * P + u * P // 2, t * P + (u + 1) * P // 2)

@@ -252,8 +252,9 @@ def tile_picked_lora_gelu_po_kernel(
         quantise_h(LAST)
         nc.scalar.copy(y_pairs[0][:, 1:2, :], first[1][:])
         store_y(0, low)
-        nc.scalar.copy(y_pairs[0][:, 2:3, :], first[2][:])
-        nc.scalar.copy(y_pairs[0][:, 3:4, :], first[3][:])
+        for c in range(2):
+            for t in range(2, PACK):
+                nc.scalar.copy(y_pairs[0][:, t, chunk_tokens(c)], first[t][:, 0, chunk_tokens(c)])
         store_y(0, high)
 
         last = [open_piece("pre%d" % (2 + t), 1, slice(t, t + 1), both) for t in range(2)]
@@ -268,9 +269,9 @@ def tile_picked_lora_gelu_po_kernel(
         store_y(1, high)
         for c in range(2):
             round_y(c, slice(0, PACK))
+        quantise_y(0)
         round_y(3, low)
         round_y(2, slice(0, PACK))
-        quantise_y(0)
         quantise_y(1)
         nc.scalar.copy(
             y_bf[3][:].rearrange("p (n t) -> p n t", t=PACK)[:, :, high], last[3][:].rearrange("p t n -> p n t")

@@ -23,7 +23,6 @@ CHUNK = 128
 CHUNKS = S // CHUNK
 LAST = CHUNKS - 1
 ON_GPSIMD = 3
-WARM_UPS = 4
 
 
 def tile_picked_lora_gelu_po_kernel(
@@ -107,17 +106,6 @@ def tile_picked_lora_gelu_po_kernel(
                     w2_cols[u][:].rearrange("p j (m t) -> p m j t", t=PACK)[:, :, :, first : first + slices],
                 )
                 if first > 0:
-                    spare = psum.tile([P, CHUNK], F32, name="spare", tag="pre3")
-                    for i in range(WARM_UPS):
-                        nc.tensor.matmul_mx(
-                            out=spare[:],
-                            lhsT=w2_codes[:, :P].bitcast(FP8X4),
-                            lhsT_scale=w2_plane[:, :P],
-                            rhs=w2_codes[:, :P].bitcast(FP8X4),
-                            rhs_scale=w2_plane[:, :P],
-                            start=True,
-                            stop=True,
-                        )
                     x_codes = gather_words(0, 1)
                 for t in range(first, first + slices):
                     cols = slice(t * P + u * P // 2, t * P + (u + 1) * P // 2)

@@ -34,12 +34,12 @@ def tile_picked_lora_gelu_po_kernel(
         psum = ctx.enter_context(tc.psum_pool(name="psum", bufs=1))
 
         def sbuf(name, shape, dtype, tag=None):
-            return keep.tile(shape, dtype, name=name, tag=tag or name, align_bytes=64)
+            return keep.tile(shape, dtype, name=name, tag=tag or name, align_bytes=256)
 
         late = ctx.enter_context(tc.tile_pool(name="late", bufs=1))
 
         def placed(name, shape, dtype, offset):
-            return late.tile(shape, dtype, name=name, tag=name, align_bytes=64, offset=offset)
+            return late.tile(shape, dtype, name=name, tag=name, align_bytes=256, offset=offset)
 
         def live_rows(q):
             return slice(32 * q, 32 * q + 4)

from contextlib import ExitStack

import concourse.mybir as mybir

K, T, S, H = 512, 1024, 512, 512
FLOPS = 3 * 2 * K * H * S

F32 = mybir.dt.float32
BF16 = mybir.dt.bfloat16
I32 = mybir.dt.int32
U32 = mybir.dt.uint32
U16 = mybir.dt.uint16
U8 = mybir.dt.uint8
FP8X4 = mybir.dt.float8_e4m3fn_x4
FP4X4 = mybir.dt.float4_e2m1fn_x4
GELU = mybir.ActivationFunctionType.Gelu_apprx_tanh

P = 128
PACK = 4
QUADRANTS = 4
LIST_ROWS = 16
CHUNK = 128
CHUNKS = S // CHUNK
LAST = CHUNKS - 1
ON_GPSIMD = 3


def tile_picked_lora_gelu_po_kernel(
    tc, x_words, x_scales, w1_words, w1_scales, w2, w3_words, w3_scales, offs, out_0, out_1, out_2
):
    nc = tc.nc
    with ExitStack() as ctx:
        keep = ctx.enter_context(tc.tile_pool(name="keep", bufs=1))
        psum = ctx.enter_context(tc.psum_pool(name="psum", bufs=1))

        def sbuf(name, shape, dtype, tag=None):
            return keep.tile(shape, dtype, name=name, tag=tag or name, align_bytes=256)

        late = ctx.enter_context(tc.tile_pool(name="late", bufs=1))

        def placed(name, shape, dtype, offset):
            return late.tile(shape, dtype, name=name, tag=name, align_bytes=256, offset=offset)

        def live_rows(q):
            return slice(32 * q, 32 * q + 4)

        def scale_rows(q):
            return slice(4 * q, 4 * q + 4)

        def chunk_tokens(c):
            return slice(c * CHUNK, (c + 1) * CHUNK)

        offsets = keep.tile([P, S // LIST_ROWS], U16, name="offsets")
        x_table = sbuf("x_table", [P, T], I32)
        x_scale_table = sbuf("x_scale_table", [P, T], U8)
        w2_cols = [sbuf("w2_cols%d" % u, [P, PACK, H // 2], F32) for u in range(2)]
        w_raw = [sbuf("w_raw%d" % w, [P, 2 * H], U8) for w in range(2)]
        w_scales = placed("w_scales", [P, 4 * H], U8, 1024)[:, : 2 * H]

        nc.vector.memset(x_scale_table[:].bitcast(I32), 0)
        nc.gpsimd.memset(w_scales[:].bitcast(I32), 0)

        def load_weight_scales(queue, w, q):
            rows = w_scales[live_rows(q), :].bitcast(I32).rearrange("p (u w c) -> p u w c", u=2, w=2)
            scales = (w1_scales, w3_scales)[w]
            queue.dma_start(rows[:, :, w, :], scales[0, scale_rows(q), :].bitcast(I32).rearrange("p (u c) -> p u c", u=2))

        w2_view = w2.rearrange("(p j) c -> p j c", j=PACK)
        weight_quadrants = [(w, q) for w in range(2) for q in range(QUADRANTS)]
        for w, q in weight_quadrants[:ON_GPSIMD]:
            load_weight_scales(nc.gpsimd, w, q)
        nc.sync.dma_start(w2_cols[0][:], w2_view[:, :, : H // 2])
        nc.sync.dma_start(offsets[:], offs)
        for q in range(QUADRANTS):
            nc.sync.dma_start(x_scale_table[live_rows(q), :].bitcast(I32), x_scales[0, scale_rows(q), :].bitcast(I32))
        nc.sync.dma_start(w2_cols[1][:], w2_view[:, :, H // 2 :])
        nc.sync.dma_start(x_table[:], x_words[0].rearrange("p n r -> p (n r)").bitcast(I32))
        nc.sync.dma_start(w_raw[0][:].bitcast(I32), w1_words[0].bitcast(I32))
        for w, q in weight_quadrants[ON_GPSIMD:]:
            load_weight_scales(nc.sync, w, q)
        nc.sync.dma_start(w_raw[1][:].bitcast(I32), w3_words[0].bitcast(I32))

        warm = sbuf("warm", [P, 1], F32)
        nc.scalar.activation(warm[:], w2_cols[0][:, 0, 0:1], GELU)

        x_pair = sbuf("x_pair", [P, 2 * CHUNK], U32)
        x_rest = sbuf("x_rest", [P, 2 * CHUNK], U32)

        def gather_words(first, count):
            codes = (x_pair, x_rest)[first // 2][:, first % 2 * CHUNK : (first % 2 + count) * CHUNK]
            entries = slice(first * CHUNK // LIST_ROWS, (first + count) * CHUNK // LIST_ROWS)
            nc.vector.tensor_copy(codes, x_table[:].bitcast(U32).indirect(offsets[:, entries]))
            return [codes[:, chunk_tokens(c)] for c in range(count)]

        x_plane = sbuf("x_plane", [P, S], U8)
        nc.vector.tensor_copy(x_plane[:], x_scale_table[:].indirect(offsets[:]))

        w2_codes = sbuf("w2_codes", [P, H], U32)
        w2_plane = sbuf("w2_plane", [P, H], U8, "x_scale_table")
        for u in range(2):
            slices = PACK // (u + 1)
            for first in range(0, PACK, slices):
                w2_bf = sbuf("w2_bf%d_%d" % (u, first), [P, slices * H // 2], BF16)
                nc.scalar.copy(
                    w2_bf[:].rearrange("p (t m j) -> p m j t", t=slices, j=PACK),
                    w2_cols[u][:].rearrange("p j (m t) -> p m j t", t=PACK)[:, :, :, first : first + slices],
                )
                if first > 0:
                    x_codes = gather_words(0, 1)
                for t in range(first, first + slices):
                    cols = slice(t * P + u * P // 2, t * P + (u + 1) * P // 2)
                    nc.vector.quantize_mx(
                        out=w2_codes[:, cols].bitcast(FP8X4),
                        scales=w2_plane[:, cols],
                        in_=w2_bf[:, (t - first) * H // 2 : (t - first + 1) * H // 2],
                    )

        x_codes = x_codes + gather_words(1, 1) + gather_words(2, 2)

        w_dealt = [sbuf("w_dealt%d" % w, [P, PACK, 2 * P], U8) for w in range(2)]

        def deal_words(copy, w):
            copy(
                w_dealt[w][:].bitcast(U16).rearrange("p t (g m) -> p g t m", m=8),
                w_raw[w][:].bitcast(U16).rearrange("p (g m t) -> p g t m", m=8, t=PACK),
            )

        deal_words(nc.scalar.copy, 0)
        w_plane = sbuf("w_plane", [P, 2, PACK, P], U8)

        def deal_weights():
            for u in range(2):
                nc.vector.tensor_copy(
                    w_plane[:, :, :, u * P // 2 : (u + 1) * P // 2].rearrange("p w t (g m) -> p w g t m", m=16),
                    w_scales[:, u * H : (u + 1) * H].rearrange("p (w g m t) -> p w g t m", w=2, m=16, t=PACK),
                )
            deal_words(nc.vector.tensor_copy, 1)

        def hidden(c):
            pre = psum.tile([P, PACK, CHUNK], F32, name="pre%d" % c, tag="pre%d" % c)
            for t in range(PACK):
                cols = slice(t * P, (t + 1) * P)
                nc.tensor.matmul_mx(
                    out=pre[:, t, :],
                    lhsT=w2_codes[:, cols].bitcast(FP8X4),
                    lhsT_scale=w2_plane[:, cols],
                    rhs=x_codes[c].bitcast(FP8X4),
                    rhs_scale=x_plane[:, chunk_tokens(c)],
                    start=True,
                    stop=True,
                )
            if c == 2:
                deal_weights()
            if c >= 2:
                activated = placed("h_bf%d" % c, [P, CHUNK * PACK], BF16, 1024 * c - 512)
            else:
                activated = sbuf("h_bf%d" % c, [P, CHUNK * PACK], BF16)
            nc.scalar.activation(
                activated[:].rearrange("p (n t) -> p n t", t=PACK), pre[:].rearrange("p t n -> p n t"), GELU
            )
            return activated

        h_bf = [hidden(c) for c in range(CHUNKS)]

        def weight_passes(bank, w, codes, plane, slices, opener=0):
            per_bank = len(slices)
            for place, t in enumerate(slices):
                nc.tensor.matmul_mx(
                    out=bank[:, place, :],
                    lhsT=w_dealt[w][:, t, :].bitcast(FP4X4),
                    lhsT_scale=w_plane[:, w, t, :],
                    rhs=codes.bitcast(FP8X4),
                    rhs_scale=plane,
                    start=w == opener and place == 0,
                    stop=w != opener and place == per_bank - 1,
                )

        h_planes = [sbuf("h_plane%d" % u, [P, 2 * CHUNK], U8)[:] for u in range(2)]
        x_planes = [x_plane[:, : 2 * CHUNK], x_plane[:, 2 * CHUNK :]]
        h_pairs = [placed("h_pair0", [P, 2 * CHUNK], U32, 512), sbuf("h_pair1", [P, 2 * CHUNK], U32)]
        x_pairs = [x_pair, x_rest]
        y_pairs = [sbuf("y_pair%d" % u, [P, PACK, 2 * CHUNK], F32) for u in range(2)]
        y_bf = [sbuf("y_bf%d" % c, [P, CHUNK * PACK], BF16) for c in range(CHUNKS)]
        y_codes = sbuf("y_codes", [P, S], I32)
        y_plane = sbuf("y_plane", [P, S], U8)
        out_view = out_0.rearrange("(p t) n -> p t n", t=PACK)
        codes_view = out_1[0].rearrange("p n r -> p (n r)").bitcast(I32)

        def quantise_h(c):
            nc.vector.quantize_mx(
                out=h_pairs[c // 2][:, chunk_tokens(c % 2)].bitcast(FP8X4),
                scales=h_planes[c // 2][:, chunk_tokens(c % 2)],
                in_=h_bf[c][:],
            )

        def open_piece(tag, pair, rows, local):
            bank = psum.tile(
                [P, rows.stop - rows.start, local.stop - local.start],
                F32,
                name="acc%d_%d_%d" % (pair, rows.start, local.start),
                tag=tag,
            )
            slices = range(rows.start, rows.stop)
            weight_passes(bank, 0, x_pairs[pair][:, local], x_planes[pair][:, local], slices)
            return bank, h_pairs[pair][:, local], h_planes[pair][:, local], slices

        def close_piece(bank, codes, plane, slices):
            weight_passes(bank, 1, codes, plane, slices)
            return bank

        def store_y(pair, rows):
            nc.sync.dma_start(out_view[:, rows, 2 * CHUNK * pair : 2 * CHUNK * (pair + 1)], y_pairs[pair][:, rows, :])

        def round_y(c, rows):
            nc.vector.tensor_copy(
                y_bf[c][:].rearrange("p (g i t) -> p g t i", i=4, t=PACK)[:, :, rows],
                y_pairs[c // 2][:, rows, chunk_tokens(c % 2)].rearrange("p t (g i) -> p g t i", i=4),
            )

        def quantise_y(c):
            tokens = chunk_tokens(c)
            nc.vector.quantize_mx(out=y_codes[:, tokens].bitcast(FP8X4), scales=y_plane[:, tokens], in_=y_bf[c][:])

        both, low, high = slice(0, 2 * CHUNK), slice(0, 2), slice(2, 4)
        for c in range(LAST):
            quantise_h(c)
        def late_piece(tag, c):
            bank = psum.tile([P, 2, CHUNK], F32, name="late%d" % c, tag=tag)
            local = chunk_tokens(c % 2)
            weight_passes(bank, 1, h_pairs[1][:, local], h_planes[1][:, local], range(2, PACK), 1)
            weight_passes(bank, 0, x_pairs[1][:, local], x_planes[1][:, local], range(2, PACK), 1)
            return bank

        first = [open_piece("acc%d" % t, 0, slice(t, t + 1), both) for t in range(LAST)]
        first = [close_piece(*piece) for piece in first]
        first.append(psum.tile([P, 1, 2 * CHUNK], F32, name="first3", tag="acc3"))
        weight_passes(first[LAST], 1, h_pairs[0][:], h_planes[0], [LAST], 1)
        weight_passes(first[LAST], 0, x_pairs[0][:], x_planes[0], [LAST], 1)
        nc.vector.tensor_copy(y_pairs[0][:, 0:1, :], first[0][:])
        quantise_h(LAST)
        nc.scalar.copy(y_pairs[0][:, 1:2, :], first[1][:])
        store_y(0, low)
        for c in range(2):
            for t in range(2, PACK):
                nc.scalar.copy(y_pairs[0][:, t, chunk_tokens(c)], first[t][:, 0, chunk_tokens(c)])
        store_y(0, high)

        last = [open_piece("pre%d" % (2 + t), 1, slice(t, t + 1), both) for t in range(2)]
        fourth = open_piece("acc0", 1, high, chunk_tokens(1))
        last = [close_piece(*piece) for piece in last]
        last = last + [late_piece("pre0", 2), close_piece(*fourth)]
        for t in range(2):
            nc.scalar.copy(y_pairs[1][:, t : t + 1, :], last[t][:])
        store_y(1, low)
        nc.vector.tensor_copy(y_pairs[1][:, high, chunk_tokens(0)], last[2][:])
        nc.scalar.copy(y_pairs[1][:, high, chunk_tokens(1)], last[3][:])
        store_y(1, high)
        for c in range(2):
            round_y(c, slice(0, PACK))
        quantise_y(0)
        round_y(3, low)
        round_y(2, slice(0, PACK))
        quantise_y(1)
        nc.scalar.copy(
            y_bf[3][:].rearrange("p (n t) -> p n t", t=PACK)[:, :, high], last[3][:].rearrange("p t n -> p n t")
        )
        quantise_y(3)
        quantise_y(2)

        nc.sync.dma_start(codes_view, y_codes[:])
        for q in range(QUADRANTS):
            queue = nc.scalar if q % 2 == 0 else nc.sync
            queue.dma_start(out_2[0, scale_rows(q), :].bitcast(I32), y_plane[live_rows(q), :].bitcast(I32))
